import numpy as np, ml_dtypes
CORES = [5,29,101,125,133,157,229,253]
N = 8
BF = ml_dtypes.bfloat16
def f(rng, *shape):
    return (rng.standard_normal(shape, dtype=np.float32) * np.exp2(rng.integers(-2, 3, shape[:-1] + (1,)))).astype(BF)
def wide(rng, *shape):
    v = f(rng, *shape).astype(np.float32); k = shape[:-2] + (1, shape[-1])
    return (v * np.exp2(rng.integers(-6, 7, k)) * (rng.random(k) > 0.0625)).astype(BF)
W, L, T, C, TH, SH = 4096, 128, 4, 6, 11, 12
def at(tab, a):
    return np.take_along_axis(tab, a.reshape(tab.shape[:-1] + (-1,)), -1).reshape(a.shape)
def tax(rng, key):
    term = np.argsort(key, axis=-1); gap = W - 1 - np.argsort(term, axis=-1)
    def up(lo, hi):
        v = np.where(rng.random((N, 8, W)) < 0.75, rng.random((1, 8, W)), rng.random((N, 8, W)))
        return np.take_along_axis(np.broadcast_to(term, (N, 8, W)), W - 1 - (gap * (lo + (hi - lo) * v)).astype(np.int64), 2)
    return term, gap, up(0.3, 0.7), up(0.05, 0.4)
def heights(rng, gap):
    h = (1.5 * (SH - np.log2(gap + 1.0))).astype(np.float32)[None, :, None, :]
    e = (h + rng.standard_normal((N, 8, 16, W), dtype=np.float32)) * np.exp2(rng.integers(-2, 3, (N, 8, 16, 1))).astype(np.float32)
    return e.reshape(N, 128, W).astype(BF)
def low(rng, term, n, top):
    return np.take_along_axis(np.broadcast_to(term, (N, 8, W)), rng.integers(0, top, (N, 8, n)), 2)
def lanes(rng, term, p0, p1):
    s = low(rng, term, 16 * L, W // 2).reshape(N, 8, 16, L)
    z = np.where(rng.random((N, 8, 16 * T * L)) < 0.1, low(rng, term, 16 * T * L, W), low(rng, term, 16 * T * L, W // 2)).reshape(N, 8, 16, T, L)
    kind = rng.integers(0, 8, (N, 8, 1, L))
    d = np.where(kind < 4, rng.integers(2, C + 1, s.shape), rng.integers(1, C + 1, s.shape)); d = np.where((kind < 3) & (rng.random(s.shape) < 0.1), 1, d)
    a = s
    for i in range(C):
        nx = at(p0, a)
        if i == 0: nx = np.where(rng.random(s.shape) < 0.4, at(p1, a), nx)
        a = np.where(d > i, nx, a)
    g = np.where(kind == 7, low(rng, term, 16 * L, W).reshape(s.shape), a)
    return s, g, z, (rng.random((N, 8, T, L)) < 0.4).astype(np.int64)
def pack(e, pa, s, g, z, sg):
    i4 = lambda v, *sh: np.ascontiguousarray(np.reshape(v, (N,) + sh)).astype(np.int32)
    return {"ev": np.reshape(e, (N, 128, W)).astype(BF), "par": i4(pa, 8, W), "s0": i4(s, 128, L), "g0": i4(g, 128, L), "z": i4(z, 128, T * L), "sg": i4(sg, 8, T * L)}
def setup_inputs(rng):
    term, gap, p0, p1 = tax(rng, rng.random((8, W)))
    return pack(heights(rng, gap), p0 + W * p1, *lanes(rng, term, p0, p1))
def setup_inputs_corners(rng):
    term, gap, p0, p1 = tax(rng, rng.random((8, W))); own = np.arange(W); c = rng.integers(0, 7, (1, 8, W))
    p0 = np.where(c == 0, own, np.where((c == 1) | (c == 4), W - 1, np.where((c == 2) | (c == 3), 0, p0)))
    p1 = np.where((c == 0) | (c == 3), own, np.where(c == 1, W - 1, np.where((c == 2) | (c == 4), 0, p1)))
    b = np.where(np.arange(N)[:, None, None] == 0, own, W - 1); p0 = np.where(c == 6, b, p0); p1 = np.where(c == 6, b, p1)
    for p in (p0, p1): p[:, ::2, W - 1] = W - 1; p[:, 1::2, W - 1] = 0
    e = heights(rng, gap).astype(np.float32); e[:, :, 0] = -256.0; e[:, :, W - 1] = 256.0
    s, g, z, sg = lanes(rng, term, p0, p1); one = (N, 8, 1, L)
    n = rng.choice(np.array([0, 0, 1, 4, 5, 16]), one); k = np.argsort(rng.random(s.shape), axis=2)
    g = np.where(rng.random(one) < 0.8, np.where(k < n, 0, W - 1), g)
    same = rng.random(one) < 0.2; s = np.where(same, s[:, :, :1], s); z = np.where(same[:, :, :, None], z[:, :, :1], z)
    g = np.where(rng.random(one) < 0.08, s, g); m = rng.integers(0, 8, (N, 8, 1, T, L))
    z = np.where(m == 0, s[:, :, :, None], np.where((m == 1) & (rng.random(z.shape) < 0.5), W - 1, np.where((m == 2) & (rng.random(z.shape) < 0.3), 0, z)))
    sg[0, :, 0] = 0; sg[1, :, 0] = 1; sg[2, :, 0] = 1; g[0] = W - 1
    for h in range(8):
        o = np.nonzero(c[0, h, 1:W - 1] == 0)[0] + 1; v = np.nonzero(c[0, h, 1:W - 1] == 6)[0] + 1
        s[0, h] = np.where(rng.random((1, L)) < 0.4, rng.choice(o, (16, L)), rng.choice(v, (16, L)))
        a, u = rng.permutation(v)[:2]; w = e[:, 16 * h:16 * h + 16]
        w[1:, :, a] = w[1:, :, u]; w[1, rng.permutation(16)[TH:], a] = -256.0
        j = np.append(rng.permutation(L - 1)[:L // 8], L - 1); i = rng.integers(0, 16, j.size)
        s[0, h, :, j] = rng.choice(o, (j.size, 16)); s[0, h, i, j] = a; z[0, h, i, 0, j] = u
    s[2, 7, :, L - 1] = rng.choice(o, 16); g[2, 7, :, L - 1] = W - 1; sg[2, 7, 0, L - 1] = 0
    for h in range(8):
        o = np.nonzero(c[0, h, 1:W - 1] == 0)[0] + 1; j = L if h < 7 else 1
        s[N - 1, h, :, :j] = rng.choice(o, (16, j)); g[N - 1, h, :, :j] = W - 1; sg[N - 1, h, 0] = 1; sg[N - 1, h, 0, :j] = 0
    return pack(e, p0 + W * p1, s, g, z, sg)
def setup_inputs_ends(rng):
    term, gap, p0, p1 = tax(rng, rng.random((8, W))); e = heights(rng, gap).astype(np.float32).reshape(N, 8, 16, W)
    cnt = rng.choice(np.array([0, 16, 8, 7, TH, TH - 1]), (N, 8, 1)); cnt[:, 0] = 16; cnt[:, 7] = 0
    v = np.where(np.argsort(rng.random((N, 8, 16)), axis=2) < cnt, 32.0, -32.0); v[:, 3] = 0.0
    e[..., 0] = v; e[..., W - 1] = -v
    pa = np.where(rng.random((N, 8, W)) < 0.85, (W * W - 1) * rng.integers(0, 2, (N, 8, W)), p0 + W * p1)
    kind = rng.integers(0, 5, (N, 8)); kind[:, 0] = 0; kind[:, 7] = 0; kind[N - 1] = 2
    pa[:, :, 0] = np.array([W * W - 1, 0, W * W - 1, 0, W - 1])[kind]; pa[:, :, W - 1] = np.array([0, W * W - 1, W * W - 1, 0, W * (W - 1)])[kind]
    def ends(*t):
        sh = (N, 8, 16) + t + (L,); one = (N, 8, 1) + t + (L,)
        x = np.where(rng.random(one) < 0.5, (W - 1) * rng.integers(0, 2, one), (W - 1) * rng.integers(0, 2, sh))
        return np.where((rng.random(one) < 0.25) & (rng.random(sh) < 0.5), rng.integers(0, W, sh), x)
    s = ends(); g = ends(); z = ends(T); sg = rng.integers(0, 2, (N, 8, T, L))
    x = (W - 1) * rng.integers(0, 2, (8, 16, L)); s[N - 1] = x; g[N - 1] = x; z[N - 1, :, :, 0] = x; sg[N - 1, :, 0] = 0; sg[1, :, 0] = 1
    s[:N - 1, 7, :, L - 3:] = 0; g[:N - 1, 7, :, L - 2:] = W - 1; g[:N - 1, 7, :, L - 3] = 0
    z[:N - 1, 7, :, 0, L - 3:] = W - 1; z[:N - 1, 7, :15, 0, L - 1] = 0; sg[:N - 1, 7, 0, L - 3:] = np.array([1, 0, 0])
    return pack(e, pa, s, g, z, sg)
def setup_inputs_spread(rng):
    c = rng.integers(-6, 7, (8, W)); term, gap, p0, p1 = tax(rng, c + rng.random((8, W)))
    w = np.abs(wide(rng, N, 128, W).astype(np.float32)).reshape(N, 8, 16, W) * np.exp2(2.0 * c).astype(np.float32)[None, :, None, :]
    w = np.where(rng.random((N, 8, 16, 1)) < 0.06, -w, w)
    return pack(w, p0 + W * p1, *lanes(rng, term, p0, p1))
def setup_inputs_ties(rng):
    term, gap, p0, p1 = tax(rng, rng.random((8, W))); q = W // 8; top = gap < q
    x = rng.integers(0, 4, (N, 8, 16, W)); x = np.where(top[None, :, None, :] & (rng.random(x.shape) < 0.75), 3, x)
    x[:, 5] = x[:, 5] // 2; x[:, 2] = 1
    u = np.take_along_axis(term[:, W - q:], rng.integers(0, q, (8, W)), 1)[None]
    p0 = np.where(rng.random((N, 8, W)) < 0.9, u, p0); p1 = np.where(rng.random((1, 8, W)) < 0.6, p0, p1)
    s, g, z, sg = lanes(rng, term, p0, p1); g = np.where(rng.random((N, 8, 1, L)) < 0.7, at(p0, s), g)
    return pack(x.astype(np.float32), p0 + W * p1, s, g, z, sg)
def check_inputs(d):
    bad = []
    for k, hi in (("par", W * W - 1), ("s0", W - 1), ("g0", W - 1), ("z", W - 1), ("sg", 1)):
        if np.min(d[k]) < 0 or np.max(d[k]) > hi: bad.append("range of " + k)
    e = d["ev"].astype(np.float32)
    if not np.all(np.isfinite(e)): bad.append("ev is not finite")
    if np.any((e != 0) & (np.abs(e) < np.float32(2.0 ** -126))): bad.append("ev holds subnormal numbers")
    return bad
def wits(tab, a):
    return np.take_along_axis(tab, a.reshape(8, 1, -1), 2).reshape(8, 16, 16, L)
def reference(ev, par, s0, g0, z, sg):
    e = ev.astype(np.float32).reshape(N, 8, 16, W); pa = par.astype(np.int64); p0 = pa & (W - 1); p1 = pa >> SH
    zs = z.astype(np.int64).reshape(N, 8, 16, T, L); plus = sg.reshape(N, 8, T, L) == 1
    S = s0.astype(np.int64).reshape(N, 8, 16, L); G = g0.astype(np.int64).reshape(N, 8, 16, L)
    ride = np.zeros((N, 8, L), bool); rz = np.zeros((N, 8, 16, L), np.int64)
    for t in range(T):
        for r in range(N):
            q = (r + t) % N; th = TH + (int(np.sum(ride[r])) & 1)
            x = np.where(ride[r][:, None], rz[r], zs[q, :, :, t]); pos = (plus[q, :, t] & ~ride[r])[:, None]
            ex = wits(e[q], x); g = G[r]; a = S[r]
            miss = np.sum(np.sum(wits(e[q], g) >= ex, axis=1) < th, axis=1)[:, None]
            for i in range(C):
                cov = np.sum(wits(e[q], a) >= ex, axis=1)
                nx = np.where(cov >= 8, at(p0[q], a), at(p1[q], a))
                stop = np.where(pos, cov >= th, nx == g)
                a = np.where(stop, a, nx)
            full = ~pos & (miss == 0); can = full & stop & (cov < th)
            win = np.argmin(np.where(can, cov, 99), axis=1)
            hit = can & (np.arange(16)[None, :, None] == win[:, None])
            S[r] = np.where(pos, a, S[r]); G[r] = np.where((pos & (miss > 4)) | hit, a, g)
            ride[r] = full[:, 0] & ~np.any(can, axis=1); rz[r] = x
    return {"ys": S.reshape(N, 128, L).astype(np.float32), "yg": G.reshape(N, 128, L).astype(np.float32)}

@@ -1,0 +1,522 @@
+import math
+from concourse.mybir import dt, AluOpType, AxisListType, ActivationFunctionType
+
+A_ = AluOpType
+F_ = ActivationFunctionType
+NV, NC, L2, STEPS = 4, 2, 64, 6
+NPV, NPS = 2, 2
+XV = (0,)
+ALPHA = 0.8318
+TOP = 86.0
+E11, E12 = [math.exp(TOP - 16 * ALPHA * _th) for _th in (11, 12)]
+
+SCRATCH = {
+    "tev": ("sbuf", [128, 4096], "bfloat16"), "ptab": ("sbuf", [128, 4096], "bfloat16"),
+    "pc": ("sbuf", [128, 256], "int32"), "ti": ("sbuf", [128, 256], "int32"),
+    "dgi": ("sbuf", [128, 6 * 256], "int32"), "dg": ("sbuf", [128, 6 * 256], "bfloat16"),
+    "zi": ("sbuf", [128, 512], "int32"), "zf": ("sbuf", [128, 512], "float32"),
+    "sgi": ("sbuf", [128, 512], "int32"), "sgb": ("sbuf", [128, 512], "bfloat16"), "sgl": ("sbuf", [128, 512], "bfloat16"),
+    "si": ("sbuf", [128, 128], "int32"), "gi": ("sbuf", [128, 128], "int32"),
+    "inm": ("sbuf", [128, 10 * 192], "uint16"), "som": ("sbuf", [128, 8 * 192], "uint16"),
+    "rxm": ("sbuf", [128, 8 * 64], "uint16"), "oxm": ("sbuf", [128, 8 * 64], "uint16"),
+    "thb": ("sbuf", [128, 16], "float32"), "cnt": ("sbuf", [128, 8], "float32"), "cni": ("sbuf", [128, 16], "int32"),
+    "yo": ("sbuf", [128, 256], "float32"),
+    "pcol": ("sbuf", [128, 16], "int32"), "fcol": ("sbuf", [128, 32], "float32"),
+    "itf": ("sbuf", [128, 144], "float32"), "itg": ("sbuf", [128, 128], "float32"), "it8": ("sbuf", [128, 8], "float32"),
+    "itk": ("sbuf", [128, 8, 8], "float32"),
+    "bo": ("sbuf", [128, 2, 8], "bfloat16"), "wp": ("sbuf", [128, 3, 8], "bfloat16"),
+    "cna": ("sbuf", [128, 2, 8, 8], "bfloat16"), "cnb": ("sbuf", [128, 8, 8], "bfloat16"),
+    "c128": ("sbuf", [128, 8, 8], "bfloat16"), "cg": ("sbuf", [128, 64], "float32"),
+    "ch0": ("sbuf", [128, 64], "float32"), "ch1": ("sbuf", [128, 64], "float32"),
+    "cb0": ("sbuf", [128, 64], "bfloat16"), "cb1": ("sbuf", [128, 64], "bfloat16"),
+    "blk": ("sbuf", [128, 128], "bfloat16"), "idb": ("sbuf", [128, 128], "bfloat16"),
+    "one": ("sbuf", [128, 128], "bfloat16"), "w0": ("sbuf", [128, 144], "bfloat16"), "r8": ("sbuf", [128, 128], "bfloat16"),
+    "vsl": ("psum", [128, 512], "float32"), "gl": ("psum", [128, 512], "float32"),
+}
+for _c in "AB":
+    SCRATCH.update({
+        "sgf" + _c: ("sbuf", [128, 128], "float32"), "rxf" + _c: ("sbuf", [128, 64], "float32"),
+        "drz" + _c: ("sbuf", [128, 64], "float32"), "om" + _c: ("sbuf", [128, 64], "bfloat16"),
+        "xf" + _c: ("sbuf", [128, 64], "float32"),
+        "ex" + _c: ("sbuf", [128, 1024], "bfloat16"), "ge" + _c: ("sbuf", [128, 1024], "bfloat16"),
+        "gg" + _c: ("sbuf", [128, 1024], "bfloat16"), "gp" + _c: ("sbuf", [128, 1024], "bfloat16"),
+        "off" + _c: ("sbuf", [128, 64], "uint16"),
+        "cz" + _c: ("sbuf", [128, 2, 8, 8], "float32"), "tu" + _c: ("sbuf", [128, 8, 8], "float32"),
+        "rr" + _c: ("sbuf", [128, 8, 8], "float32"),
+        "zz" + _c: ("sbuf", [128, 17, 8], "float32"), "zk" + _c: ("sbuf", [128, 17, 8], "bfloat16"),
+        "pos" + _c: ("sbuf", [128, 64], "float32"), "p2" + _c: ("sbuf", [128, 64], "bfloat16"),
+        "nq" + _c: ("sbuf", [128, 64, 2], "bfloat16"), "pg" + _c: ("sbuf", [128, 64, 2], "float32"),
+        "mi" + _c: ("sbuf", [128, 64], "bfloat16"), "fu" + _c: ("sbuf", [128, 64], "float32"),
+        "pu" + _c: ("sbuf", [128, 64], "float32"), "nf" + _c: ("sbuf", [128, 64], "bfloat16"),
+        "mx" + _c: ("sbuf", [128, 8, 8], "float32"), "ww" + _c: ("sbuf", [128, 64], "bfloat16"),
+        "hit" + _c: ("sbuf", [128, 64], "float32"), "upd" + _c: ("sbuf", [128, 64], "float32"),
+        "nc" + _c: ("sbuf", [128, 64], "float32"), "st" + _c: ("sbuf", [128, 192], "float32"),
+        "cv" + _c: ("psum", [128, 8, 8, 8], "float32"), "pa" + _c: ("psum", [128, 8, 8, 8], "float32"),
+        "tr" + _c: ("psum", [128, 512], "float32"),
+    })
+NDMA = 24
+SEMAPHORES = ["v", "s", "p", "q", "loc"] + ["d%d" % i for i in range(NDMA)] \
+    + ["arr%d%s" % (t, c) for t in range(1, 5) for c in "AB"] + ["xar%d%s" % (t, c) for t in range(1, 4) for c in "AB"]
+
+CYC, PEC, LAT = 1.04e-3, 0.75e-3, 0.10
+
+
+def gath(n):
+    return 0.06 + 1.55 * CYC * n
+
+
+def small(n):
+    return max(64, n) * CYC
+
+
+def routes(core, dst, topo):
+    if topo.may_write(core, dst):
+        return [core, core]
+    own = [c for c in topo.cores_of(core) if c != core and topo.may_write(c, dst)]
+    own.sort(key=lambda c: topo.die(c) != topo.die(core))
+    return [own[0], own[1]]
+
+
+def build(T):
+    ops = []
+    nd = [0]
+
+    def op(eng, cost, R, W, fn, bank=None, lat=0.0, out=0.0):
+        ops.append({"e": eng, "c": cost, "R": R, "W": W, "f": fn, "b": bank, "lat": lat})
+        return len(ops) - 1
+
+    def v(cost, R, W, fn, bank=None):
+        return op("v", cost, R, W, fn, bank)
+
+    def dma(queue, R, W, o, i, dur):
+        k = nd[0]
+        nd[0] += 1
+        ops.append({"e": queue, "c": 0.1, "R": R, "W": W, "b": None, "lat": dur, "dsem": "d%d" % k,
+                    "f": (lambda q, o=o, i=i: q.dma_start(o, i))})
+
+    def ts(out, in0, s1, o0, s2=None, o1=None):
+        if o1 is None:
+            return lambda q: q.tensor_scalar(out, in0, s1, None, o0)
+        return lambda q: q.tensor_scalar(out, in0, s1, s2, o0, o1)
+
+    def tt(out, a, b, o):
+        return lambda q: q.tensor_tensor(out, a, b, o)
+
+    def cp(out, a):
+        return lambda q: q.tensor_copy(out, a)
+
+    def act(out, a, f, bias=0.0, scale=1.0):
+        return lambda q: q.activation(out, a, f, bias=bias, scale=scale)
+
+    def mms(lst):
+        def f(q):
+            r = None
+            n = len(lst)
+            for i, (o, a, b) in enumerate(lst):
+                r = q.matmul(o, a, b, i == 0, i == n - 1)
+            return r
+        return f
+
+    def mmk(lst):
+        def f(q):
+            r = None
+            for o, a, b in lst:
+                r = q.matmul(o, a, b, True, True)
+            return r
+        return f
+
+    dma("y", [], ["zi"], T.zi[:], T.z[:], 3.0)
+    dma("y", [], ["pc"], T.pc[:], T.par[:], 2.5)
+    dma("s", [], ["sgi"], T.sgi[0:8, :], T.sg[:], 2.0)
+    dma("s", [], ["si"], T.si[:], T.s0[:], 2.0)
+    dma("s", [], ["gi"], T.gi[:], T.g0[:], 2.0)
+    dma("y", [], ["tev0"], T.tev[0:64, :], T.ev[0:64, :], 6.0)
+    dma("y", [], ["tev1"], T.tev[64:128, :], T.ev[64:128, :], 6.0)
+
+    fl = True
+    op("g", 0.2, [], ["pcol0"], lambda q: q.iota(T.pcol[:, 0:1], [[0, 1]], 0, 1))
+    op("g", 0.6, [], ["ti"], lambda q: q.iota(T.ti[:], [[1, 256]], 0, 256))
+    op("g", 0.4, [], ["itf"], lambda q: q.iota(T.itf[:], [[1, 144]], 0, 0, allow_small_or_imprecise_dtypes=fl))
+    op("g", 0.4, [], ["itg"], lambda q: q.iota(T.itg[:], [[1, 8], [0, 16]], 0, 0, allow_small_or_imprecise_dtypes=fl))
+    op("g", 0.2, [], ["it8"], lambda q: q.iota(T.it8[:], [[1, 8]], 0, 0, allow_small_or_imprecise_dtypes=fl))
+    op("g", 0.3, [], ["itk"], lambda q: q.iota(T.itk[:], [[1, 8], [0, 8]], 0, 0, allow_small_or_imprecise_dtypes=fl))
+    v(small(2048), [], ["ptab%d" % d for d in range(6)], lambda q: q.memset(T.ptab[:], 0.0))
+
+    def icol(j, src, *a):
+        v(small(1), ["pcol%d" % src], ["pcol%d" % j], ts(T.pcol[:, j:j + 1], T.pcol[:, src:src + 1], *a))
+    icol(1, 0, 4, A_.arith_shift_right)
+    icol(2, 0, 7, A_.bitwise_and)
+    icol(3, 0, 3, A_.arith_shift_right, 1, A_.bitwise_and)
+    icol(4, 0, 1, A_.arith_shift_right)
+    icol(5, 0, 1, A_.bitwise_and)
+    icol(6, 0, 1, A_.arith_shift_right, 7, A_.bitwise_and)
+    icol(7, 0, 15, A_.bitwise_and)
+    v(small(8), ["pcol%d" % j for j in range(8)], ["fc"], cp(T.fcol[:, 0:8], T.pcol[:, 0:8]))
+    FC = lambda j: T.fcol[:, j:j + 1]
+
+    def fcol(j, in0, s1, o0, s2=None, o1=None, dep=()):
+        v(small(1), ["fc"] + list(dep), ["fc%d" % j], ts(FC(j), in0, s1, o0, s2, o1))
+    fcol(8, FC(1), 8.0, A_.mult, FC(2), A_.add)
+    fcol(9, FC(5), -1000.0, A_.mult, FC(4), A_.add)
+    fcol(10, FC(5), 1000.0, A_.mult, FC(4), A_.add)
+    fcol(11, FC(10), -1000.0, A_.add, dep=["fc10"])
+    fcol(12, FC(1), 16.0, A_.mult, 16.0, A_.add)
+    fcol(13, FC(3), -1.0, A_.mult, 1.0, A_.add)
+    fcol(14, FC(7), -ALPHA, A_.mult, TOP - 64 * 16 * ALPHA, A_.add)
+    fcol(15, FC(6), 0.0, A_.is_equal)
+    fcol(16, FC(6), 1.0, A_.is_equal)
+    fcol(20, FC(6), 2.0, A_.is_equal, 2.0, A_.mult)
+    v(small(1), ["fc15", "fc16"], ["fc18"], tt(FC(18), FC(15), FC(16), A_.subtract))
+    v(small(1), ["fc15", "fc16"], ["fc19"], tt(FC(19), FC(15), FC(16), A_.add))
+    for o in range(2):
+        v(small(8), ["it8", "fc"], ["bo"], ts(T.bo[:, o], T.it8[:], FC(1), A_.is_equal, 1.0 - 2.0 * o, A_.mult))
+    for o in range(3):
+        v(small(8), ["it8", "fc", "fc%d" % (18 + o)], ["wp"], ts(T.wp[:, o], T.it8[:], FC(1), A_.is_equal, FC(18 + o), A_.mult))
+    v(small(64), [], ["cna"], lambda q: q.memset(T.cna[:, 0], 0.0))
+    v(small(64), ["itk", "fc"], ["cna"], ts(T.cna[:, 1], T.itk[:], FC(1), A_.is_equal, 2.0, A_.mult))
+    v(small(64), ["itk", "fc"], ["cnb"], ts(T.cnb[:], T.itk[:], FC(1), A_.is_equal, -512.0, A_.mult))
+    v(small(64), [], ["c128"], lambda q: q.memset(T.c128[:], 128.0))
+    v(small(64), ["itf", "fc8"], ["cg"], ts(T.cg[:], T.itf[:, 0:64], FC(8), A_.is_equal))
+    v(small(64), ["itf", "fc9"], ["ch0"], ts(T.ch0[:], T.itf[:, 0:64], FC(9), A_.is_equal))
+    v(small(64), ["itf", "fc11"], ["ch1"], ts(T.ch1[:], T.itf[:, 0:64], FC(11), A_.is_equal))
+    v(small(64), ["itf", "fc9"], ["cb0"], ts(T.cb0[:], T.itf[:, 0:64], FC(9), A_.is_equal))
+    v(small(64), ["itf", "fc11"], ["cb1"], ts(T.cb1[:], T.itf[:, 0:64], FC(11), A_.is_equal))
+    v(small(128), ["itg", "fc"], ["blk"], ts(T.blk[:], T.itg[:], FC(1), A_.is_equal))
+    v(small(128), ["itf", "fc", "pcol0"], ["idb"], ts(T.idb[:], T.itf[:, 0:128], FC(0), A_.is_equal))
+    v(small(128), ["itg", "fc"], ["r8"], ts(T.r8[:], T.itg[:], FC(0), A_.is_equal))
+    v(small(144), ["itf", "fc12"], ["w0"], ts(T.w0[:], T.itf[:], FC(12), A_.is_equal))
+    v(small(64), [], ["one"], lambda q: q.memset(T.one[:], 1.0))
+    for j, x in enumerate((11.0, 21.5, 1.5 * E11, 2.0 * E11)):
+        v(small(1), [], ["th0%d" % j], (lambda x, j: lambda q: q.memset(T.thb[:, j:j + 1], x))(x, j))
+    op("s", 0.1, ["th00"], ["warm"], act(T.fcol[:, 24:25], T.thb[:, 0:1], F_.Exp))
+    for c in "AB":
+        v(small(136), [], ["zz" + c], (lambda c: lambda q: q.memset(T["zz" + c][:], 0.0))(c))
+        v(small(68), [], ["zk" + c], (lambda c: lambda q: q.memset(T["zk" + c][:], 0.0))(c))
+
+    DI = lambda d: T.dgi[:, 256 * d:256 * d + 256]
+    DG = lambda d: T.dg[:, 256 * d:256 * d + 256]
+    for d in (4, 5, 0, 1, 2, 3):
+        src, nm = (T.ti, "ti") if d > 3 else (T.pc, "pc")
+        sh = 6 * (d % 4) if d < 4 else 6 * (d - 4)
+        if sh:
+            v(small(256), [nm], ["dgi%d" % d], ts(DI(d), src[:], sh, A_.arith_shift_right, 63, A_.bitwise_and))
+        else:
+            v(small(256), [nm], ["dgi%d" % d], ts(DI(d), src[:], 63, A_.bitwise_and))
+        v(small(256), ["dgi%d" % d], ["dg%d" % d], ts(DG(d), DI(d), 0.5 if d % 2 == 0 else 32.0, A_.mult))
+        dma("y", ["dg%d" % d], ["ptab%d" % d], T.ptab[d::16, :], DG(d), 2.5)
+    PT = ["ptab%d" % d for d in range(6)]
+    EV = ["tev0", "tev1"]
+
+    v(small(512), ["sgi"], ["sgb"], cp(T.sgb[0:8, :], T.sgi[0:8, :]))
+    op("p", 0.3, ["r8", "sgb"], ["vsl"], lambda q: q.matmul(T.vsl[:], T.r8[0:8, :], T.sgb[0:8, :], True, True), "vsl")
+    v(small(512), ["vsl"], ["sgl"], cp(T.sgl[:], T.vsl[:]), "vsl")
+    v(small(512), ["zi"], ["zf"], cp(T.zf[:], T.zi[:]))
+
+    def slot(t, ci):
+        return 192 * (2 * t + ci)
+
+    for t in range(NV):
+        for ci, c in enumerate("AB"):
+            B = lambda n, c=c: T[n + c]
+            lanes = slice(L2 * ci, L2 * ci + L2)
+            tl = slice(128 * t + L2 * ci, 128 * t + L2 * ci + L2)
+            q0 = slot(t, ci)
+            IS, IG, IR = T.inm[:, q0:q0 + 64], T.inm[:, q0 + 64:q0 + 128], T.inm[:, q0 + 128:q0 + 192]
+            OX = T.oxm[:, 64 * (2 * t + ci):64 * (2 * t + ci) + 64]
+            RX = T.rxm[:, 64 * (2 * t + ci):64 * (2 * t + ci) + 64]
+            kS, kG, kR, kO = ["%s%d%s" % (n, t, c) for n in ("iS", "iG", "iR", "ox")]
+            if t == 0:
+                v(small(64), ["zf"], [kO], cp(OX, T.zf[:, tl]))
+                v(small(64), ["si"], [kS], cp(IS, T.si[:, lanes]))
+                v(small(64), ["gi"], [kG], cp(IG, T.gi[:, lanes]))
+                v(small(64), ["sgl"], ["pos" + c], cp(B("pos")[:], T.sgl[:, tl]))
+            else:
+                kX = "rx%d%s" % (t, c)
+                v(small(64), [kX], ["rxf" + c], cp(B("rxf")[:], RX))
+                v(small(128), ["rxf" + c, "zf"], ["drz" + c], tt(B("drz")[:], B("rxf")[:], T.zf[:, tl], A_.subtract))
+                v(small(64), [kR], ["om" + c], ts(B("om")[:], IR, -1.0, A_.mult, 1.0, A_.add))
+                vx = T.vsl[:, 256 * ci + 128:256 * ci + 192]
+                v(small(128), ["om" + c, "drz" + c], ["va" + c], tt(vx, B("om")[:], B("drz")[:], A_.mult), "vsl")
+                v(small(64), ["va" + c, "rxf" + c], ["xf" + c], tt(B("xf")[:], B("rxf")[:], vx, A_.subtract), "vsl")
+                v(small(64), ["xf" + c], [kO], cp(OX, B("xf")[:]))
+                v(small(128), ["om" + c, "sgl"], ["pos" + c], tt(B("pos")[:], B("om")[:], T.sgl[:, tl], A_.mult))
+            if t < NV - 1:
+                op("net", 1.2, [kO], ["rx%d%s" % (t + 1, c)], ("x", t + 1, ci, OX), None, 6.0)
+            op("s", gath(512), EV + [kO], ["exs" + c], act(B("ex")[:, 512:1024], T.tev[:].indirect(OX[:, 32:64]), F_.Copy))
+            if ci in XV:
+                v(gath(512), EV + [kO], ["exv" + c], cp(B("ex")[:, 0:512], T.tev[:].indirect(OX[:, 0:32])))
+            else:
+                op("s", gath(512), EV + [kO], ["exv" + c], act(B("ex")[:, 0:512], T.tev[:].indirect(OX[:, 0:32]), F_.Copy))
+            v(small(64), [kS], ["Sf" + c], cp(B("sgf")[:, 0:64], IS))
+            v(small(64), [kG], ["Gf" + c], cp(B("sgf")[:, 64:128], IG))
+            for h in range(2):
+                op("s", 0.07, ["pos" + c], ["nq" + c], act(B("nq")[:, :, h], B("pos")[:], F_.Copy, 2.0, -1.0))
+                v(small(64), [kG, "fc13"], ["pg" + c], ts(B("pg")[:, :, h], IG, FC(13) if h == 0 else FC(3), A_.mult))
+            op("s", 0.07, ["pos" + c], ["p2" + c], act(B("p2")[:], B("pos")[:], F_.Copy, 0.0, 2.0))
+            op("p", 384 * PEC, ["pg" + c, "cg", "nq" + c, "cnb", "one", "c128"], ["gE" + c],
+               mms([(B("pa")[:, 3], B("pg")[:], T.cg[:]), (B("pa")[:, 3], B("nq")[:], T.cnb[:]), (B("pa")[:, 3], T.one[:], T.c128[:])]), "pa" + c)
+        if t > 0:
+            op("p", 0.1, ["omA", "omB", "one"], ["par"],
+               mms([(T.trA[:, 320:384], T.one[:], T.omA[:]), (T.trA[:, 320:384], T.one[:], T.omB[:])]), "trA")
+            v(small(64), ["par"], ["cnt"], lambda q, t=t: q.tensor_reduce(T.cnt[:, t:t + 1], T.trA[:, 320:384], AxisListType.X, A_.add), "trA")
+            v(small(1), ["cnt"], ["cni"], cp(T.cni[:, t:t + 1], T.cnt[:, t:t + 1]))
+            v(small(1), ["cni"], ["cnj"], ts(T.cni[:, 8 + t:9 + t], T.cni[:, t:t + 1], 16, A_.bitwise_and))
+            TB = lambda j, t=t: T.thb[:, 4 * t + j:4 * t + j + 1]
+            for j, (m, b) in ((1, (-0.0625, 21.5)), (0, (0.0625, 11.0))):
+                v(small(1), ["cnj"], ["th%d%d" % (t, j)], ts(TB(j), T.cni[:, 8 + t:9 + t], m, A_.mult, b, A_.add))
+            for j, m in ((2, 1.5), (3, 2.0)):
+                k = "th%d%d" % (t, j)
+                v(small(1), ["cnj"], [k], ts(TB(j), T.cni[:, 8 + t:9 + t], -m * E11 / 16, A_.mult, m * E11, A_.add))
+                v(small(1), [k], [k], ts(TB(j), TB(j), m * E12, A_.max))
+        TH = lambda j, t=t: T.thb[:, 4 * t + j:4 * t + j + 1]
+        for i in range(STEPS):
+            for ci, c in enumerate("AB"):
+                B = lambda n, c=c: T[n + c]
+                q0 = slot(t, ci)
+                off, kF = (T.inm[:, q0:q0 + 64], "iS%d%s" % (t, c)) if i == 0 else (B("off"), "off" + c)
+                for j in range(NPS):
+                    w = 64 // NPS
+                    op("s", gath(16 * w), PT + [kF], ["gp" + c],
+                       act(B("gp")[:, 16 * w * j:16 * w * j + 16 * w], T.ptab[:].indirect(off[:, w * j:w * j + w]), F_.Copy))
+                for j in range(NPV):
+                    w = 64 // NPV
+                    sl = slice(16 * w * j, 16 * w * j + 16 * w)
+                    v(gath(16 * w), EV + [kF, "exs" + c, "exv" + c], ["ge" + c],
+                      tt(B("ge")[:, sl], T.tev[:].indirect(off[:, w * j:w * j + w]), B("ex")[:, sl], A_.is_ge))
+                op("p", 512 * PEC, ["gp" + c, "wp"], ["pa" + c],
+                   mmk([(B("pa")[:, 0:3, :, k], B("gp")[:, k::8], T.wp[:]) for k in range(8)]), "pa" + c)
+                op("p", 640 * PEC, ["nq" + c, "cna", "ge" + c, "bo"], ["cv" + c],
+                   mms([(B("cv")[:, 0:2], B("nq")[:], T.cna[:])] + [(B("cv")[:, 0:2, :, k], B("ge")[:, k::8], T.bo[:]) for k in range(8)]), "cv" + c)
+                op("s", 0.08, ["cv" + c], ["cz0" + c], act(B("cz")[:, 0], B("cv")[:, 0], F_.Sign, -7.5), "cv" + c)
+                op("s", 0.08, ["cv" + c, "th%d1" % t], ["cz1" + c], act(B("cz")[:, 1], B("cv")[:, 1], F_.Sign, TH(1), -1.0), "cv" + c)
+                VE, VD = T.vsl[:, 256 * ci:256 * ci + 64], T.vsl[:, 256 * ci + 64:256 * ci + 128]
+                v(small(64), ["cz0" + c, "pa" + c], ["tu" + c], tt(B("tu")[:], B("cz")[:, 0], B("pa")[:, 0], A_.mult), "pa" + c)
+                v(small(64), ["tu" + c, "pa" + c], ["rr" + c], tt(B("rr")[:], B("tu")[:], B("pa")[:, 1], A_.add), "pa" + c)
+                v(small(64), ["rr" + c, "gE" + c], ["ve" + c], tt(VE, B("rr")[:], B("pa")[:, 3], A_.is_equal), "pa" + c)
+                v(small(64), ["rr" + c, "pa" + c], ["vd" + c], tt(VD, B("pa")[:, 2], B("rr")[:], A_.subtract), "pa" + c)
+                v(small(64), ["ve" + c, "cz1" + c], ["mx" + c], tt(B("mx")[:], B("cz")[:, 1], VE, A_.max))
+                v(small(64), ["mx" + c, "vd" + c], ["vm" + c], tt(VE, B("mx")[:], VD, A_.mult))
+                v(small(64), ["rr" + c, "vm" + c], ["zz" + c], tt(B("zz")[:, 1::2, :], B("rr")[:], VE, A_.add))
+                if i == STEPS - 1:
+                    v(small(64), ["mx" + c, "cv" + c], ["zk" + c], tt(B("zk")[:, 1::2, :], B("mx")[:], B("cv")[:, 1], A_.mult), "cv" + c)
+                op("p", 512 * PEC, ["zz" + c, "ch0", "ch1"], ["aL" + c],
+                   mms([(B("tr")[:, 0:64], B("zz")[:, 1:17, :], T.ch0[:]), (B("tr")[:, 0:64], B("zz")[:, 0:16, :], T.ch1[:])]), "tr" + c)
+                if i < STEPS - 1:
+                    v(small(64), ["aL" + c], ["off" + c], cp(B("off")[:], B("tr")[:, 0:64]), "tr" + c)
+            if i == 0:
+                for ci, c in enumerate("AB"):
+                    B = lambda n, c=c: T[n + c]
+                    q0 = slot(t, ci) + 64
+                    for j in range(NPV):
+                        w = 64 // NPV
+                        sl = slice(16 * w * j, 16 * w * j + 16 * w)
+                        v(gath(16 * w), EV + ["iG%d%s" % (t, c), "exs" + c, "exv" + c], ["gg" + c],
+                          tt(B("gg")[:, sl], T.tev[:].indirect(T.inm[:, q0 + w * j:q0 + w * j + w]), B("ex")[:, sl], A_.is_ge))
+                    CG, FM = T.gl[:, 128 * ci:128 * ci + 64], T.gl[:, 128 * ci + 64:128 * ci + 128]
+                    op("p", 1024 * PEC, ["gg" + c, "w0"], ["cG" + c],
+                       mms([(CG, T.w0[:, 16 - k:144 - k], B("gg")[:, k::16]) for k in range(16)]), "gl")
+                    v(small(64), ["cG" + c, "th%d0" % t], ["mi" + c], ts(B("mi")[:], CG, TH(0), A_.is_lt), "gl")
+                    op("p", 0.1, ["mi" + c, "p2" + c, "blk"], ["fm" + c],
+                       mms([(FM, T.blk[:], B("mi")[:]), (FM, T.blk[:], B("p2")[:])]), "gl")
+                    v(small(64), ["fm" + c], ["fu" + c], ts(B("fu")[:], FM, 0.0, A_.is_equal), "gl")
+                    v(small(64), ["fm" + c], ["pu" + c], ts(B("pu")[:], FM, 36.0, A_.is_gt), "gl")
+                    v(small(64), ["fm" + c], ["nf" + c], ts(B("nf")[:], FM, 0.0, A_.is_gt, -64.0, A_.mult), "gl")
+        for ci, c in enumerate("AB"):
+            B = lambda n, c=c: T[n + c]
+            bk, bg = "tr" + c, "gl"
+            KL, MM, AL = T.gl[:, 256 + 128 * ci:320 + 128 * ci], T.gl[:, 320 + 128 * ci:384 + 128 * ci], B("tr")[:, 0:64]
+            va, vb, vm = [T.vsl[:, 256 * ci + 64 * j:256 * ci + 64 * j + 64] for j in (2, 3, 0)]
+            Sf, Gf = B("sgf")[:, 0:64], B("sgf")[:, 64:128]
+            so = T.som[:, slot(t, ci):slot(t, ci) + 192]
+            kM = "so%d%s" % (t, c)
+            op("p", 0.15, ["zk" + c, "nf" + c, "cb0", "cb1", "idb"], ["kL" + c],
+               mms([(KL, B("zk")[:, 1:17, :], T.cb0[:]), (KL, B("zk")[:, 0:16, :], T.cb1[:]), (KL, T.idb[:], B("nf")[:])]), bg)
+            op("s", 0.08, ["kL" + c, "fc14"], ["ww" + c], act(B("ww")[:], KL, F_.Exp, FC(14), 16 * ALPHA), bg)
+            op("p", 0.1, ["ww" + c, "blk"], ["MM" + c], mms([(MM, T.blk[:], B("ww")[:])]), bg)
+            v(small(64), ["MM" + c, "th%d2" % t], ["ve" + c], ts(vm, MM, 0.5, A_.mult, TH(2), A_.max), bg)
+            if t < NV - 1:
+                v(small(64), ["MM" + c, "th%d3" % t], ["nc" + c], ts(B("nc")[:], MM, TH(3), A_.is_lt), bg)
+            v(small(64), ["aL" + c, "Sf" + c], ["va" + c], tt(va, AL, Sf, A_.subtract), bk)
+            v(small(64), ["va" + c, "pos" + c], ["va" + c], tt(va, B("pos")[:], va, A_.mult))
+            v(small(64), ["va" + c, "Sf" + c], ["stS" + c], tt(B("st")[:, 0:64], Sf, va, A_.add))
+            v(small(64), ["stS" + c], [kM + "S"], cp(so[:, 0:64], B("st")[:, 0:64]))
+            v(small(64), ["aL" + c, "Gf" + c], ["vb" + c], tt(vb, AL, Gf, A_.subtract), bk)
+            v(small(64), ["ve" + c, "ww" + c], ["hit" + c], tt(B("hit")[:], B("ww")[:], vm, A_.is_gt))
+            v(small(128), ["hit" + c, "pu" + c], ["upd" + c], tt(B("upd")[:], B("hit")[:], B("pu")[:], A_.add))
+            if t < NV - 1:
+                v(small(128), ["nc" + c, "fu" + c], ["stR" + c], tt(B("st")[:, 128:192], B("nc")[:], B("fu")[:], A_.mult))
+            v(small(64), ["upd" + c, "vb" + c], ["vb" + c], tt(vb, B("upd")[:], vb, A_.mult))
+            v(small(64), ["vb" + c, "Gf" + c], ["stG" + c], tt(B("st")[:, 64:128], Gf, vb, A_.add))
+            nw = 192 if t < NV - 1 else 128
+            v(small(nw - 64), ["stG" + c] + (["stR" + c] if t < NV - 1 else []), [kM], cp(so[:, 64:nw], B("st")[:, 64:nw]))
+            op("net", 1.2, [kM, kM + "S"], ["%s%d%s" % (n, t + 1, c) for n in ("iS", "iG", "iR")],
+               ("m", t + 1, ci, so[:, 0:nw]), None, 6.0)
+    for ci, c in enumerate("AB"):
+        q0 = slot(NV, ci)
+        for j in range(2):
+            v(small(64), ["iS4" + c], ["yo%d%s" % (j, c)], cp(T.yo[:, 128 * j + 64 * ci:128 * j + 64 * ci + 64], T.inm[:, q0 + 64 * j:q0 + 64 * j + 64]))
+            dma("ys"[j], ["yo%d%s" % (j, c)], [], (T.ys, T.yg)[j][:, 64 * ci:64 * ci + 64], T.yo[:, 128 * j + 64 * ci:128 * j + 64 * ci + 64], 2.0)
+    return ops
+
+
+def link(ops):
+    wr, rd, base, bank = {}, {}, {}, {}
+    for n, o in enumerate(ops):
+        d = set()
+        for k in o["R"]:
+            d.update(wr.get(k, ()))
+        for k in o["W"]:
+            old = wr.get(k, [])
+            piece = old and k not in o["R"] and not rd.get(k) and all(ops[m]["e"] == o["e"] and ops[m]["W"] == o["W"] for m in old)
+            if piece:
+                wr[k] = old + [n]
+            else:
+                base[k] = set(old) | set(rd.get(k, ()))
+                wr[k] = [n]
+                rd[k] = []
+            d.update(base[k])
+        if o["b"]:
+            sg = bank.get(o["b"])
+            if not sg or sg["e"] != o["e"]:
+                sg = bank[o["b"]] = {"e": o["e"], "n": [], "pre": set(sg["n"]) if sg else set()}
+            d.update(sg["pre"])
+            sg["n"].append(n)
+        d.discard(n)
+        o["D"] = sorted(d)
+        for k in o["R"]:
+            if k not in o["W"]:
+                rd.setdefault(k, []).append(n)
+    return ops
+
+
+def order(ops):
+    n = len(ops)
+    suc = [[] for _ in ops]
+    pri = [0.0] * n
+    need = [len(o["D"]) for o in ops]
+    for i, o in enumerate(ops):
+        for d in o["D"]:
+            suc[d].append(i)
+    for i in range(n - 1, -1, -1):
+        o = ops[i]
+        pri[i] = o["c"] + o["lat"] + LAT + max([pri[j] for j in suc[i]] or [0.0])
+    free, ready, est, done, seq = {}, [], [0.0] * n, [0.0] * n, []
+    ready = [i for i in range(n) if not need[i]]
+    q = lambda e: "g" if e == "net" else e
+    while ready:
+        tm = min(max(est[i], free.get(q(ops[i]["e"]), 0.0)) for i in ready)
+        first = min((max(est[i], free.get(q(ops[i]["e"]), 0.0)), -pri[i], i) for i in ready)
+        eng = q(ops[first[2]]["e"])
+        cand = [i for i in ready if q(ops[i]["e"]) == eng and max(est[i], free.get(eng, 0.0)) <= tm + 0.02]
+        b = max(cand, key=lambda i: (pri[i], -i))
+        s = max(est[b], free.get(eng, 0.0))
+        free[eng] = s + ops[b]["c"]
+        done[b] = s + ops[b]["c"] + ops[b]["lat"]
+        ready.remove(b)
+        seq.append(b)
+        for j in suc[b]:
+            need[j] -= 1
+            est[j] = max(est[j], done[b] + LAT)
+            if not need[j]:
+                ready.append(j)
+    return seq
+
+
+def emit(g, core, T, topo, ops, seq, nxt, home):
+    qs = {"v": g.vector, "s": g.scalar, "p": g.tensor, "g": g, "net": g, "y": g.sync}
+    cs = {"v": "v", "s": "s", "p": "p", "g": "q"}
+    known = {e: {} for e in "vspgy"}
+    count = {}
+    loc = 0
+    for n in seq:
+        o = ops[n]
+        e = "g" if o["e"] == "net" else o["e"]
+        q, kn = qs[e], known[e]
+        for d in o["D"]:
+            for sem, val, clk in ops[d]["sig"]:
+                if kn.get(sem, 0) < val:
+                    q.wait_ge(T.sem[sem], val)
+                    kn[sem] = val
+                    for k2, v2 in clk.items():
+                        if kn.get(k2, 0) < v2:
+                            kn[k2] = v2
+        if o["e"] == "net":
+            kind, t, ci, src = o["f"]
+            dst = home if t == NV else nxt
+            via = routes(core, dst, topo)[ci]
+            to = dst if via == core else via
+            sem = ("arr%d%s" if kind == "m" else "xar%d%s") % (t, "AB"[ci])
+            wide = 192 if kind == "m" else 64
+            w = 128 if kind == "m" and t == NV else wide
+            at = wide * (2 * t + ci)
+            land = (T.inm if kind == "m" else T.rxm)[:, at:at + w]
+            rid, pid = topo.addr(to, core)
+            g.remote_dma(land, src, T.sem[sem], T.sem.loc, pid, rid, topo.mask(core, to))
+            loc += len(topo.engines(core, to))
+            o["sig"] = [(sem, last_hop(T, core, t, kind, ci, topo), {})]
+        elif "dsem" in o:
+            o["f"](q).then_inc(T.sem[o["dsem"]], 16)
+            o["sig"] = [(o["dsem"], 16, dict(kn))]
+        else:
+            sem = cs[e]
+            count[sem] = count.get(sem, 0) + 1
+            o["f"](q).then_inc(T.sem[sem], 1)
+            clk = dict(kn)
+            clk[sem] = count[sem]
+            o["sig"] = [(sem, count[sem], clk)]
+    for o in ops:
+        if "dsem" in o:
+            g.wait_ge(T.sem[o["dsem"]], 16)
+    for sem, val in count.items():
+        g.wait_ge(T.sem[sem], val)
+    g.wait_ge(T.sem.loc, loc)
+
+
+def ends(rank, T, kind, t):
+    n = len(T.cores)
+    return (rank - (NV - 1)) % n if t == NV else (rank + 1) % n
+
+
+def last_hop(T, core, t, kind, ci, topo):
+    rank, n = T.rank_of(core), len(T.cores)
+    src = T.cores[(rank + (NV - 1)) % n] if t == NV else T.cores[(rank - 1) % n]
+    via = routes(src, core, topo)[ci]
+    return len(topo.engines(via, core))
+
+
+def relay(g, core, T, topo):
+    jobs = []
+    for rank, src in enumerate(T.cores):
+        if core not in topo.cores_of(src):
+            continue
+        for t in range(1, NV + 1):
+            dst = T.cores[ends(rank, T, "m", t)]
+            for ci in range(NC):
+                if routes(src, dst, topo)[ci] == core:
+                    if t < NV:
+                        jobs.append((src, dst, t, 0, ci))
+                    jobs.append((src, dst, t, 1, ci))
+    jobs.sort(key=lambda j: (j[2], j[3], j[4]))
+    loc = 0
+    for src, dst, t, m, ci in jobs:
+        wide = 192 if m else 64
+        w = 128 if m and t == NV else wide
+        at = wide * (2 * t + ci)
+        sem = T.sem[("arr%d%s" if m else "xar%d%s") % (t, "AB"[ci])]
+        buf = (T.inm if m else T.rxm)[:, at:at + w]
+        g.wait_ge(sem, len(topo.engines(src, core)))
+        rid, pid = topo.addr(dst, core)
+        g.remote_dma(buf, buf, sem, T.sem.loc, pid, rid, topo.mask(core, dst))
+        loc += len(topo.engines(core, dst))
+    if loc:
+        g.wait_ge(T.sem.loc, loc)
+
+
+def rank_program(g, core, T, topo):
+    rank = T.rank_of(core)
+    if rank is None:
+        relay(g, core, T, topo)
+        return
+    ops = link(build(T))
+    seq = order(ops)
+    emit(g, core, T, topo, ops, seq, T.cores[ends(rank, T, "m", 1)], T.cores[ends(rank, T, "m", NV)])

@@ -4,7 +4,7 @@ from concourse.mybir import dt, AluOpType, AxisListType, ActivationFunctionType
 A_ = AluOpType
 F_ = ActivationFunctionType
 NV, NC, L2, STEPS = 4, 2, 64, 6
-NPV, NPS = 2, 2
+CUT_A, CUT_B, CUT_G, CUT_P0, CUT_P = (32, 32), (32, 32), (32, 32), (32, 32), (64,)
 XV = (0,)
 ALPHA = 0.8318
 TOP = 86.0
@@ -42,7 +42,7 @@ for _c in "AB":
         "gg" + _c: ("sbuf", [128, 1024], "bfloat16"), "gp" + _c: ("sbuf", [128, 1024], "bfloat16"),
         "off" + _c: ("sbuf", [128, 64], "uint16"),
         "cz" + _c: ("sbuf", [128, 2, 8, 8], "float32"), "tu" + _c: ("sbuf", [128, 8, 8], "float32"),
-        "rr" + _c: ("sbuf", [128, 8, 8], "float32"),
+        "zm" + _c: ("sbuf", [128, 17, 8], "float32"),
         "zz" + _c: ("sbuf", [128, 17, 8], "float32"), "zk" + _c: ("sbuf", [128, 17, 8], "bfloat16"),
         "pos" + _c: ("sbuf", [128, 64], "float32"), "p2" + _c: ("sbuf", [128, 64], "bfloat16"),
         "nq" + _c: ("sbuf", [128, 64, 2], "bfloat16"), "pg" + _c: ("sbuf", [128, 64, 2], "float32"),
@@ -58,11 +58,24 @@ NDMA = 24
 SEMAPHORES = ["v", "s", "p", "q", "loc"] + ["d%d" % i for i in range(NDMA)] \
     + ["arr%d%s" % (t, c) for t in range(1, 5) for c in "AB"] + ["xar%d%s" % (t, c) for t in range(1, 4) for c in "AB"]
 
-CYC, PEC, LAT = 1.04e-3, 0.75e-3, 0.10
+SHIFT = {'3Bs': 13.5, 'pBs': -0.6, '5AG': -20.6, '1As': 24.9, 'u6s': 18.4, 'u7s': -3.6, 'u9s': 29.1, 'u1s': 22.7, '5AP': 32.9,
+         'gAs': 6.3, 'fAs': -14.2, '0As': -0.8, '2AP': -40.1, 'u3s': 4.5, 'ubs': 5.8, 'u4s': 13.2, 'ues': 29.5, 'pts': 18.3,
+         'u5s': 11.1, 'uas': 9.1, '2AG': -7.5, 'uks': -5.4, 'uAs': 0.2, '1AP': 8.0, 'ups': -11.3, 'u0s': -2.0, 'u2s': -0.6,
+         'u8s': 1.2, '0BP': 14.9, 'pAs': 5.9, 'gBG': 0.4, 'gAG': -3.3, '4AP': -30.8, '0AG': -10.3, '3AG': -22.4, 'uBs': -2.3,
+         '0AS': -3.7, '3AP': 27.3}
+CYC, PEC, LAT = 1.04e-3, 0.75e-3, 0.12
 
 
 def gath(n):
     return 0.06 + 1.55 * CYC * n
+
+
+def cuts(ws):
+    out = []
+    for w in ws:
+        a = out[-1][1] if out else 0
+        out.append((a, a + w))
+    return out
 
 
 def small(n):
@@ -80,9 +93,13 @@ def routes(core, dst, topo):
 def build(T):
     ops = []
     nd = [0]
+    cur = ["u"]
 
-    def op(eng, cost, R, W, fn, bank=None, lat=0.0, out=0.0):
-        ops.append({"e": eng, "c": cost, "R": R, "W": W, "f": fn, "b": bank, "lat": lat})
+    def op(eng, cost, R, W, fn, bank=None, lat=0.0):
+        kind = "P" if eng == "p" else "s"
+        if eng in "vs" and cost > 0.45 and cur[0] != "u":
+            kind = "G" if eng == "v" else "S"
+        ops.append({"e": eng, "c": cost, "R": R, "W": W, "f": fn, "b": bank, "lat": lat, "key": cur[0] + W[0][-1] + kind})
         return len(ops) - 1
 
     def v(cost, R, W, fn, bank=None):
@@ -91,7 +108,7 @@ def build(T):
     def dma(queue, R, W, o, i, dur):
         k = nd[0]
         nd[0] += 1
-        ops.append({"e": queue, "c": 0.1, "R": R, "W": W, "b": None, "lat": dur, "dsem": "d%d" % k,
+        ops.append({"e": queue, "c": 0.1, "R": R, "W": W, "b": None, "lat": dur, "dsem": "d%d" % k, "key": "us",
                     "f": (lambda q, o=o, i=i: q.dma_start(o, i))})
 
     def ts(out, in0, s1, o0, s2=None, o1=None):
@@ -108,12 +125,12 @@ def build(T):
     def act(out, a, f, bias=0.0, scale=1.0):
         return lambda q: q.activation(out, a, f, bias=bias, scale=scale)
 
-    def mms(lst):
+    def mms(lst, first=True, last=True):
         def f(q):
             r = None
             n = len(lst)
             for i, (o, a, b) in enumerate(lst):
-                r = q.matmul(o, a, b, i == 0, i == n - 1)
+                r = q.matmul(o, a, b, first and i == 0, last and i == n - 1)
             return r
         return f
 
@@ -191,6 +208,7 @@ def build(T):
     op("s", 0.1, ["th00"], ["warm"], act(T.fcol[:, 24:25], T.thb[:, 0:1], F_.Exp))
     for c in "AB":
         v(small(136), [], ["zz" + c], (lambda c: lambda q: q.memset(T["zz" + c][:], 0.0))(c))
+        v(small(136), [], ["zm" + c], (lambda c: lambda q: q.memset(T["zm" + c][:], 0.0))(c))
         v(small(68), [], ["zk" + c], (lambda c: lambda q: q.memset(T["zk" + c][:], 0.0))(c))
 
     DI = lambda d: T.dgi[:, 256 * d:256 * d + 256]
@@ -216,6 +234,7 @@ def build(T):
         return 192 * (2 * t + ci)
 
     for t in range(NV):
+        cur[0] = "p"
         for ci, c in enumerate("AB"):
             B = lambda n, c=c: T[n + c]
             lanes = slice(L2 * ci, L2 * ci + L2)
@@ -226,7 +245,7 @@ def build(T):
             RX = T.rxm[:, 64 * (2 * t + ci):64 * (2 * t + ci) + 64]
             kS, kG, kR, kO = ["%s%d%s" % (n, t, c) for n in ("iS", "iG", "iR", "ox")]
             if t == 0:
-                v(small(64), ["zf"], [kO], cp(OX, T.zf[:, tl]))
+                v(small(64), ["zi"], [kO], cp(OX, T.zi[:, tl]))
                 v(small(64), ["si"], [kS], cp(IS, T.si[:, lanes]))
                 v(small(64), ["gi"], [kG], cp(IG, T.gi[:, lanes]))
                 v(small(64), ["sgl"], ["pos" + c], cp(B("pos")[:], T.sgl[:, tl]))
@@ -270,48 +289,48 @@ def build(T):
                 v(small(1), [k], [k], ts(TB(j), TB(j), m * E12, A_.max))
         TH = lambda j, t=t: T.thb[:, 4 * t + j:4 * t + j + 1]
         for i in range(STEPS):
+            cur[0] = str(i)
             for ci, c in enumerate("AB"):
                 B = lambda n, c=c: T[n + c]
                 q0 = slot(t, ci)
                 off, kF = (T.inm[:, q0:q0 + 64], "iS%d%s" % (t, c)) if i == 0 else (B("off"), "off" + c)
-                for j in range(NPS):
-                    w = 64 // NPS
-                    op("s", gath(16 * w), PT + [kF], ["gp" + c],
-                       act(B("gp")[:, 16 * w * j:16 * w * j + 16 * w], T.ptab[:].indirect(off[:, w * j:w * j + w]), F_.Copy))
-                for j in range(NPV):
-                    w = 64 // NPV
-                    sl = slice(16 * w * j, 16 * w * j + 16 * w)
-                    v(gath(16 * w), EV + [kF, "exs" + c, "exv" + c], ["ge" + c],
-                      tt(B("ge")[:, sl], T.tev[:].indirect(off[:, w * j:w * j + w]), B("ex")[:, sl], A_.is_ge))
+                for a, b in cuts(CUT_P0 if i == 0 else CUT_P):
+                    op("s", gath(16 * (b - a)), PT + [kF], ["gp" + c],
+                       act(B("gp")[:, 16 * a:16 * b], T.ptab[:].indirect(off[:, a:b]), F_.Copy))
+                for a, b in cuts((CUT_A, CUT_B)[ci]):
+                    v(gath(16 * (b - a)), EV + [kF, "exs" + c, "exv" + c], ["ge" + c],
+                      tt(B("ge")[:, 16 * a:16 * b], T.tev[:].indirect(off[:, a:b]), B("ex")[:, 16 * a:16 * b], A_.is_ge))
                 op("p", 512 * PEC, ["gp" + c, "wp"], ["pa" + c],
                    mmk([(B("pa")[:, 0:3, :, k], B("gp")[:, k::8], T.wp[:]) for k in range(8)]), "pa" + c)
-                op("p", 640 * PEC, ["nq" + c, "cna", "ge" + c, "bo"], ["cv" + c],
-                   mms([(B("cv")[:, 0:2], B("nq")[:], T.cna[:])] + [(B("cv")[:, 0:2, :, k], B("ge")[:, k::8], T.bo[:]) for k in range(8)]), "cv" + c)
+                op("p", 128 * PEC, ["nq" + c, "cna"], ["cw" + c], mms([(B("cv")[:, 0:2], B("nq")[:], T.cna[:])], True, False), "cv" + c)
+                op("p", 512 * PEC, ["cw" + c, "ge" + c, "bo"], ["cv" + c],
+                   mms([(B("cv")[:, 0:2, :, k], B("ge")[:, k::8], T.bo[:]) for k in range(8)], False, True), "cv" + c)
                 op("s", 0.08, ["cv" + c], ["cz0" + c], act(B("cz")[:, 0], B("cv")[:, 0], F_.Sign, -7.5), "cv" + c)
                 op("s", 0.08, ["cv" + c, "th%d1" % t], ["cz1" + c], act(B("cz")[:, 1], B("cv")[:, 1], F_.Sign, TH(1), -1.0), "cv" + c)
                 VE, VD = T.vsl[:, 256 * ci:256 * ci + 64], T.vsl[:, 256 * ci + 64:256 * ci + 128]
                 v(small(64), ["cz0" + c, "pa" + c], ["tu" + c], tt(B("tu")[:], B("cz")[:, 0], B("pa")[:, 0], A_.mult), "pa" + c)
-                v(small(64), ["tu" + c, "pa" + c], ["rr" + c], tt(B("rr")[:], B("tu")[:], B("pa")[:, 1], A_.add), "pa" + c)
-                v(small(64), ["rr" + c, "gE" + c], ["ve" + c], tt(VE, B("rr")[:], B("pa")[:, 3], A_.is_equal), "pa" + c)
-                v(small(64), ["rr" + c, "pa" + c], ["vd" + c], tt(VD, B("pa")[:, 2], B("rr")[:], A_.subtract), "pa" + c)
+                NX, MV = B("zz")[:, 1::2, :], B("zm")[:, 1::2, :]
+                v(small(64), ["tu" + c, "pa" + c], ["zz" + c], tt(NX, B("tu")[:], B("pa")[:, 1], A_.add), "pa" + c)
+                op("p", 512 * PEC, ["zz" + c, "ch0", "ch1"], ["aN" + c],
+                   mms([(B("tr")[:, 0:64], B("zz")[:, 1:17, :], T.ch0[:]), (B("tr")[:, 0:64], B("zz")[:, 0:16, :], T.ch1[:])], True, False), "tr" + c)
+                v(small(64), ["zz" + c, "gE" + c], ["ve" + c], tt(VE, NX, B("pa")[:, 3], A_.is_equal), "pa" + c)
+                v(small(64), ["zz" + c, "pa" + c], ["vd" + c], tt(VD, B("pa")[:, 2], NX, A_.subtract), "pa" + c)
                 v(small(64), ["ve" + c, "cz1" + c], ["mx" + c], tt(B("mx")[:], B("cz")[:, 1], VE, A_.max))
-                v(small(64), ["mx" + c, "vd" + c], ["vm" + c], tt(VE, B("mx")[:], VD, A_.mult))
-                v(small(64), ["rr" + c, "vm" + c], ["zz" + c], tt(B("zz")[:, 1::2, :], B("rr")[:], VE, A_.add))
+                v(small(64), ["mx" + c, "vd" + c], ["zm" + c], tt(MV, B("mx")[:], VD, A_.mult))
                 if i == STEPS - 1:
                     v(small(64), ["mx" + c, "cv" + c], ["zk" + c], tt(B("zk")[:, 1::2, :], B("mx")[:], B("cv")[:, 1], A_.mult), "cv" + c)
-                op("p", 512 * PEC, ["zz" + c, "ch0", "ch1"], ["aL" + c],
-                   mms([(B("tr")[:, 0:64], B("zz")[:, 1:17, :], T.ch0[:]), (B("tr")[:, 0:64], B("zz")[:, 0:16, :], T.ch1[:])]), "tr" + c)
+                op("p", 512 * PEC, ["zm" + c, "aN" + c, "ch0", "ch1"], ["aL" + c],
+                   mms([(B("tr")[:, 0:64], B("zm")[:, 1:17, :], T.ch0[:]), (B("tr")[:, 0:64], B("zm")[:, 0:16, :], T.ch1[:])], False, True), "tr" + c)
                 if i < STEPS - 1:
                     v(small(64), ["aL" + c], ["off" + c], cp(B("off")[:], B("tr")[:, 0:64]), "tr" + c)
             if i == 0:
+                cur[0] = "g"
                 for ci, c in enumerate("AB"):
                     B = lambda n, c=c: T[n + c]
                     q0 = slot(t, ci) + 64
-                    for j in range(NPV):
-                        w = 64 // NPV
-                        sl = slice(16 * w * j, 16 * w * j + 16 * w)
-                        v(gath(16 * w), EV + ["iG%d%s" % (t, c), "exs" + c, "exv" + c], ["gg" + c],
-                          tt(B("gg")[:, sl], T.tev[:].indirect(T.inm[:, q0 + w * j:q0 + w * j + w]), B("ex")[:, sl], A_.is_ge))
+                    for a, b in cuts(CUT_G):
+                        v(gath(16 * (b - a)), EV + ["iG%d%s" % (t, c), "exs" + c, "exv" + c], ["gg" + c],
+                          tt(B("gg")[:, 16 * a:16 * b], T.tev[:].indirect(T.inm[:, q0 + a:q0 + b]), B("ex")[:, 16 * a:16 * b], A_.is_ge))
                     CG, FM = T.gl[:, 128 * ci:128 * ci + 64], T.gl[:, 128 * ci + 64:128 * ci + 128]
                     op("p", 1024 * PEC, ["gg" + c, "w0"], ["cG" + c],
                        mms([(CG, T.w0[:, 16 - k:144 - k], B("gg")[:, k::16]) for k in range(16)]), "gl")
@@ -321,6 +340,7 @@ def build(T):
                     v(small(64), ["fm" + c], ["fu" + c], ts(B("fu")[:], FM, 0.0, A_.is_equal), "gl")
                     v(small(64), ["fm" + c], ["pu" + c], ts(B("pu")[:], FM, 36.0, A_.is_gt), "gl")
                     v(small(64), ["fm" + c], ["nf" + c], ts(B("nf")[:], FM, 0.0, A_.is_gt, -64.0, A_.mult), "gl")
+        cur[0] = "f"
         for ci, c in enumerate("AB"):
             B = lambda n, c=c: T[n + c]
             bk, bg = "tr" + c, "gl"
@@ -341,12 +361,14 @@ def build(T):
             v(small(64), ["va" + c, "Sf" + c], ["stS" + c], tt(B("st")[:, 0:64], Sf, va, A_.add))
             v(small(64), ["stS" + c], [kM + "S"], cp(so[:, 0:64], B("st")[:, 0:64]))
             v(small(64), ["aL" + c, "Gf" + c], ["vb" + c], tt(vb, AL, Gf, A_.subtract), bk)
+            vp = T.vsl[:, 256 * ci + 64:256 * ci + 128]
+            v(small(64), ["vb" + c, "pu" + c], ["vd" + c], tt(vp, B("pu")[:], vb, A_.mult))
+            v(small(64), ["vd" + c, "Gf" + c], ["upd" + c], tt(B("upd")[:], Gf, vp, A_.add))
             v(small(64), ["ve" + c, "ww" + c], ["hit" + c], tt(B("hit")[:], B("ww")[:], vm, A_.is_gt))
-            v(small(128), ["hit" + c, "pu" + c], ["upd" + c], tt(B("upd")[:], B("hit")[:], B("pu")[:], A_.add))
             if t < NV - 1:
                 v(small(128), ["nc" + c, "fu" + c], ["stR" + c], tt(B("st")[:, 128:192], B("nc")[:], B("fu")[:], A_.mult))
-            v(small(64), ["upd" + c, "vb" + c], ["vb" + c], tt(vb, B("upd")[:], vb, A_.mult))
-            v(small(64), ["vb" + c, "Gf" + c], ["stG" + c], tt(B("st")[:, 64:128], Gf, vb, A_.add))
+            v(small(64), ["hit" + c, "vb" + c], ["vb" + c], tt(vb, B("hit")[:], vb, A_.mult))
+            v(small(64), ["vb" + c, "upd" + c], ["stG" + c], tt(B("st")[:, 64:128], B("upd")[:], vb, A_.add))
             nw = 192 if t < NV - 1 else 128
             v(small(nw - 64), ["stG" + c] + (["stR" + c] if t < NV - 1 else []), [kM], cp(so[:, 64:nw], B("st")[:, 64:nw]))
             op("net", 1.2, [kM, kM + "S"], ["%s%d%s" % (n, t + 1, c) for n in ("iS", "iG", "iR")],
@@ -400,6 +422,8 @@ def order(ops):
     for i in range(n - 1, -1, -1):
         o = ops[i]
         pri[i] = o["c"] + o["lat"] + LAT + max([pri[j] for j in suc[i]] or [0.0])
+    for i in range(n):
+        pri[i] += SHIFT.get(ops[i]["key"], 0.0)
     free, ready, est, done, seq = {}, [], [0.0] * n, [0.0] * n, []
     ready = [i for i in range(n) if not need[i]]
     q = lambda e: "g" if e == "net" else e

import math
from concourse.mybir import dt, AluOpType, AxisListType, ActivationFunctionType

A_ = AluOpType
F_ = ActivationFunctionType
NV, NC, L2, STEPS = 4, 2, 64, 6
CUT_A, CUT_B, CUT_G, CUT_P0, CUT_P = (32, 32), (32, 32), (32, 32), (32, 32), (64,)
XV = (0,)
ALPHA = 0.8318
TOP = 86.0
E11, E12 = [math.exp(TOP - 16 * ALPHA * _th) for _th in (11, 12)]

SCRATCH = {
    "tev": ("sbuf", [128, 4096], "bfloat16"), "ptab": ("sbuf", [128, 4096], "bfloat16"),
    "pc": ("sbuf", [128, 256], "int32"), "ti": ("sbuf", [128, 256], "int32"),
    "dgi": ("sbuf", [128, 6 * 256], "int32"), "dg": ("sbuf", [128, 6 * 256], "bfloat16"),
    "zi": ("sbuf", [128, 512], "int32"), "zf": ("sbuf", [128, 512], "float32"),
    "sgi": ("sbuf", [128, 512], "int32"), "sgb": ("sbuf", [128, 512], "bfloat16"), "sgl": ("sbuf", [128, 512], "bfloat16"),
    "si": ("sbuf", [128, 128], "int32"), "gi": ("sbuf", [128, 128], "int32"),
    "inm": ("sbuf", [128, 10 * 192], "uint16"), "som": ("sbuf", [128, 8 * 192], "uint16"),
    "rxm": ("sbuf", [128, 8 * 64], "uint16"), "oxm": ("sbuf", [128, 8 * 64], "uint16"),
    "thb": ("sbuf", [128, 16], "float32"), "cnt": ("sbuf", [128, 8], "float32"), "cni": ("sbuf", [128, 16], "int32"),
    "yo": ("sbuf", [128, 256], "float32"),
    "pcol": ("sbuf", [128, 16], "int32"), "fcol": ("sbuf", [128, 32], "float32"),
    "itf": ("sbuf", [128, 144], "float32"), "itg": ("sbuf", [128, 128], "float32"), "it8": ("sbuf", [128, 8], "float32"),
    "itk": ("sbuf", [128, 8, 8], "float32"),
    "bo": ("sbuf", [128, 2, 8], "bfloat16"), "wp": ("sbuf", [128, 3, 8], "bfloat16"),
    "cna": ("sbuf", [128, 2, 8, 8], "bfloat16"), "cnb": ("sbuf", [128, 8, 8], "bfloat16"),
    "c128": ("sbuf", [128, 8, 8], "bfloat16"), "cg": ("sbuf", [128, 64], "float32"),
    "ch0": ("sbuf", [128, 64], "float32"), "ch1": ("sbuf", [128, 64], "float32"),
    "cb0": ("sbuf", [128, 64], "bfloat16"), "cb1": ("sbuf", [128, 64], "bfloat16"),
    "blk": ("sbuf", [128, 128], "bfloat16"), "idb": ("sbuf", [128, 128], "bfloat16"),
    "one": ("sbuf", [128, 128], "bfloat16"), "w0": ("sbuf", [128, 144], "bfloat16"), "r8": ("sbuf", [128, 128], "bfloat16"),
    "vsl": ("psum", [128, 512], "float32"), "gl": ("psum", [128, 512], "float32"),
}
for _c in "AB":
    SCRATCH.update({
        "sgf" + _c: ("sbuf", [128, 128], "float32"), "rxf" + _c: ("sbuf", [128, 64], "float32"),
        "drz" + _c: ("sbuf", [128, 64], "float32"), "om" + _c: ("sbuf", [128, 64], "bfloat16"),
        "xf" + _c: ("sbuf", [128, 64], "float32"),
        "ex" + _c: ("sbuf", [128, 1024], "bfloat16"), "ge" + _c: ("sbuf", [128, 1024], "bfloat16"),
        "gg" + _c: ("sbuf", [128, 1024], "bfloat16"), "gp" + _c: ("sbuf", [128, 1024], "bfloat16"),
        "off" + _c: ("sbuf", [128, 64], "uint16"),
        "cz" + _c: ("sbuf", [128, 2, 8, 8], "float32"), "tu" + _c: ("sbuf", [128, 8, 8], "float32"),
        "zm" + _c: ("sbuf", [128, 17, 8], "float32"),
        "zz" + _c: ("sbuf", [128, 17, 8], "float32"), "zk" + _c: ("sbuf", [128, 17, 8], "bfloat16"),
        "pos" + _c: ("sbuf", [128, 64], "float32"), "p2" + _c: ("sbuf", [128, 64], "bfloat16"),
        "nq" + _c: ("sbuf", [128, 64, 2], "bfloat16"), "pg" + _c: ("sbuf", [128, 64, 2], "float32"),
        "mi" + _c: ("sbuf", [128, 64], "bfloat16"), "fu" + _c: ("sbuf", [128, 64], "float32"),
        "pu" + _c: ("sbuf", [128, 64], "float32"), "nf" + _c: ("sbuf", [128, 64], "bfloat16"),
        "mx" + _c: ("sbuf", [128, 8, 8], "float32"), "ww" + _c: ("sbuf", [128, 64], "bfloat16"),
        "hit" + _c: ("sbuf", [128, 64], "float32"), "upd" + _c: ("sbuf", [128, 64], "float32"),
        "nc" + _c: ("sbuf", [128, 64], "float32"), "st" + _c: ("sbuf", [128, 192], "float32"),
        "cv" + _c: ("psum", [128, 8, 8, 8], "float32"), "pa" + _c: ("psum", [128, 8, 8, 8], "float32"),
        "tr" + _c: ("psum", [128, 512], "float32"),
    })
NDMA = 24
SEMAPHORES = ["v", "s", "p", "q", "loc"] + ["d%d" % i for i in range(NDMA)] \
    + ["arr%d%s" % (t, c) for t in range(1, 5) for c in "AB"] + ["xar%d%s" % (t, c) for t in range(1, 4) for c in "AB"]

SHIFT = {'3Bs': 13.5, 'pBs': -0.6, '5AG': -20.6, '1As': 24.9, 'u6s': 18.4, 'u7s': -3.6, 'u9s': 29.1, 'u1s': 22.7, '5AP': 32.9,
         'gAs': 6.3, 'fAs': -14.2, '0As': -0.8, '2AP': -40.1, 'u3s': 4.5, 'ubs': 5.8, 'u4s': 13.2, 'ues': 29.5, 'pts': 18.3,
         'u5s': 11.1, 'uas': 9.1, '2AG': -7.5, 'uks': -5.4, 'uAs': 0.2, '1AP': 8.0, 'ups': -11.3, 'u0s': -2.0, 'u2s': -0.6,
         'u8s': 1.2, '0BP': 14.9, 'pAs': 5.9, 'gBG': 0.4, 'gAG': -3.3, '4AP': -30.8, '0AG': -10.3, '3AG': -22.4, 'uBs': -2.3,
         '0AS': -3.7, '3AP': 27.3}
CYC, PEC, LAT = 1.04e-3, 0.75e-3, 0.12


def gath(n):
    return 0.06 + 1.55 * CYC * n


def cuts(ws):
    out = []
    for w in ws:
        a = out[-1][1] if out else 0
        out.append((a, a + w))
    return out


def small(n):
    return max(64, n) * CYC


def routes(core, dst, topo):
    if topo.may_write(core, dst):
        return [core, core]
    own = [c for c in topo.cores_of(core) if c != core and topo.may_write(c, dst)]
    own.sort(key=lambda c: topo.die(c) != topo.die(core))
    return [own[0], own[1]]


def build(T):
    ops = []
    nd = [0]
    cur = ["u"]

    def op(eng, cost, R, W, fn, bank=None, lat=0.0):
        kind = "P" if eng == "p" else "s"
        if eng in "vs" and cost > 0.45 and cur[0] != "u":
            kind = "G" if eng == "v" else "S"
        ops.append({"e": eng, "c": cost, "R": R, "W": W, "f": fn, "b": bank, "lat": lat, "key": cur[0] + W[0][-1] + kind})
        return len(ops) - 1

    def v(cost, R, W, fn, bank=None):
        return op("v", cost, R, W, fn, bank)

    def dma(queue, R, W, o, i, dur):
        k = nd[0]
        nd[0] += 1
        ops.append({"e": queue, "c": 0.1, "R": R, "W": W, "b": None, "lat": dur, "dsem": "d%d" % k, "key": "us",
                    "f": (lambda q, o=o, i=i: q.dma_start(o, i))})

    def ts(out, in0, s1, o0, s2=None, o1=None):
        if o1 is None:
            return lambda q: q.tensor_scalar(out, in0, s1, None, o0)
        return lambda q: q.tensor_scalar(out, in0, s1, s2, o0, o1)

    def tt(out, a, b, o):
        return lambda q: q.tensor_tensor(out, a, b, o)

    def cp(out, a):
        return lambda q: q.tensor_copy(out, a)

    def act(out, a, f, bias=0.0, scale=1.0):
        return lambda q: q.activation(out, a, f, bias=bias, scale=scale)

    def mms(lst, first=True, last=True):
        def f(q):
            r = None
            n = len(lst)
            for i, (o, a, b) in enumerate(lst):
                r = q.matmul(o, a, b, first and i == 0, last and i == n - 1)
            return r
        return f

    def mmk(lst):
        def f(q):
            r = None
            for o, a, b in lst:
                r = q.matmul(o, a, b, True, True)
            return r
        return f

    dma("y", [], ["zi"], T.zi[:], T.z[:], 3.0)
    dma("y", [], ["pc"], T.pc[:], T.par[:], 2.5)
    dma("s", [], ["sgi"], T.sgi[0:8, :], T.sg[:], 2.0)
    dma("s", [], ["si"], T.si[:], T.s0[:], 2.0)
    dma("s", [], ["gi"], T.gi[:], T.g0[:], 2.0)
    dma("y", [], ["tev0"], T.tev[0:64, :], T.ev[0:64, :], 6.0)
    dma("y", [], ["tev1"], T.tev[64:128, :], T.ev[64:128, :], 6.0)

    fl = True
    op("g", 0.2, [], ["pcol0"], lambda q: q.iota(T.pcol[:, 0:1], [[0, 1]], 0, 1))
    op("g", 0.6, [], ["ti"], lambda q: q.iota(T.ti[:], [[1, 256]], 0, 256))
    op("g", 0.4, [], ["itf"], lambda q: q.iota(T.itf[:], [[1, 144]], 0, 0, allow_small_or_imprecise_dtypes=fl))
    op("g", 0.4, [], ["itg"], lambda q: q.iota(T.itg[:], [[1, 8], [0, 16]], 0, 0, allow_small_or_imprecise_dtypes=fl))
    op("g", 0.2, [], ["it8"], lambda q: q.iota(T.it8[:], [[1, 8]], 0, 0, allow_small_or_imprecise_dtypes=fl))
    op("g", 0.3, [], ["itk"], lambda q: q.iota(T.itk[:], [[1, 8], [0, 8]], 0, 0, allow_small_or_imprecise_dtypes=fl))
    v(small(2048), [], ["ptab%d" % d for d in range(6)], lambda q: q.memset(T.ptab[:], 0.0))

    def icol(j, src, *a):
        v(small(1), ["pcol%d" % src], ["pcol%d" % j], ts(T.pcol[:, j:j + 1], T.pcol[:, src:src + 1], *a))
    icol(1, 0, 4, A_.arith_shift_right)
    icol(2, 0, 7, A_.bitwise_and)
    icol(3, 0, 3, A_.arith_shift_right, 1, A_.bitwise_and)
    icol(4, 0, 1, A_.arith_shift_right)
    icol(5, 0, 1, A_.bitwise_and)
    icol(6, 0, 1, A_.arith_shift_right, 7, A_.bitwise_and)
    icol(7, 0, 15, A_.bitwise_and)
    v(small(8), ["pcol%d" % j for j in range(8)], ["fc"], cp(T.fcol[:, 0:8], T.pcol[:, 0:8]))
    FC = lambda j: T.fcol[:, j:j + 1]

    def fcol(j, in0, s1, o0, s2=None, o1=None, dep=()):
        v(small(1), ["fc"] + list(dep), ["fc%d" % j], ts(FC(j), in0, s1, o0, s2, o1))
    fcol(8, FC(1), 8.0, A_.mult, FC(2), A_.add)
    fcol(9, FC(5), -1000.0, A_.mult, FC(4), A_.add)
    fcol(10, FC(5), 1000.0, A_.mult, FC(4), A_.add)
    fcol(11, FC(10), -1000.0, A_.add, dep=["fc10"])
    fcol(12, FC(1), 16.0, A_.mult, 16.0, A_.add)
    fcol(13, FC(3), -1.0, A_.mult, 1.0, A_.add)
    fcol(14, FC(7), -ALPHA, A_.mult, TOP - 64 * 16 * ALPHA, A_.add)
    fcol(15, FC(6), 0.0, A_.is_equal)
    fcol(16, FC(6), 1.0, A_.is_equal)
    fcol(20, FC(6), 2.0, A_.is_equal, 2.0, A_.mult)
    v(small(1), ["fc15", "fc16"], ["fc18"], tt(FC(18), FC(15), FC(16), A_.subtract))
    v(small(1), ["fc15", "fc16"], ["fc19"], tt(FC(19), FC(15), FC(16), A_.add))
    for o in range(2):
        v(small(8), ["it8", "fc"], ["bo"], ts(T.bo[:, o], T.it8[:], FC(1), A_.is_equal, 1.0 - 2.0 * o, A_.mult))
    for o in range(3):
        v(small(8), ["it8", "fc", "fc%d" % (18 + o)], ["wp"], ts(T.wp[:, o], T.it8[:], FC(1), A_.is_equal, FC(18 + o), A_.mult))
    v(small(64), [], ["cna"], lambda q: q.memset(T.cna[:, 0], 0.0))
    v(small(64), ["itk", "fc"], ["cna"], ts(T.cna[:, 1], T.itk[:], FC(1), A_.is_equal, 2.0, A_.mult))
    v(small(64), ["itk", "fc"], ["cnb"], ts(T.cnb[:], T.itk[:], FC(1), A_.is_equal, -512.0, A_.mult))
    v(small(64), [], ["c128"], lambda q: q.memset(T.c128[:], 128.0))
    v(small(64), ["itf", "fc8"], ["cg"], ts(T.cg[:], T.itf[:, 0:64], FC(8), A_.is_equal))
    v(small(64), ["itf", "fc9"], ["ch0"], ts(T.ch0[:], T.itf[:, 0:64], FC(9), A_.is_equal))
    v(small(64), ["itf", "fc11"], ["ch1"], ts(T.ch1[:], T.itf[:, 0:64], FC(11), A_.is_equal))
    v(small(64), ["itf", "fc9"], ["cb0"], ts(T.cb0[:], T.itf[:, 0:64], FC(9), A_.is_equal))
    v(small(64), ["itf", "fc11"], ["cb1"], ts(T.cb1[:], T.itf[:, 0:64], FC(11), A_.is_equal))
    v(small(128), ["itg", "fc"], ["blk"], ts(T.blk[:], T.itg[:], FC(1), A_.is_equal))
    v(small(128), ["itf", "fc", "pcol0"], ["idb"], ts(T.idb[:], T.itf[:, 0:128], FC(0), A_.is_equal))
    v(small(128), ["itg", "fc"], ["r8"], ts(T.r8[:], T.itg[:], FC(0), A_.is_equal))
    v(small(144), ["itf", "fc12"], ["w0"], ts(T.w0[:], T.itf[:], FC(12), A_.is_equal))
    v(small(64), [], ["one"], lambda q: q.memset(T.one[:], 1.0))
    for j, x in enumerate((11.0, 21.5, 1.5 * E11, 2.0 * E11)):
        v(small(1), [], ["th0%d" % j], (lambda x, j: lambda q: q.memset(T.thb[:, j:j + 1], x))(x, j))
    op("s", 0.1, ["th00"], ["warm"], act(T.fcol[:, 24:25], T.thb[:, 0:1], F_.Exp))
    for c in "AB":
        v(small(136), [], ["zz" + c], (lambda c: lambda q: q.memset(T["zz" + c][:], 0.0))(c))
        v(small(136), [], ["zm" + c], (lambda c: lambda q: q.memset(T["zm" + c][:], 0.0))(c))
        v(small(68), [], ["zk" + c], (lambda c: lambda q: q.memset(T["zk" + c][:], 0.0))(c))

    DI = lambda d: T.dgi[:, 256 * d:256 * d + 256]
    DG = lambda d: T.dg[:, 256 * d:256 * d + 256]
    for d in (4, 5, 0, 1, 2, 3):
        src, nm = (T.ti, "ti") if d > 3 else (T.pc, "pc")
        sh = 6 * (d % 4) if d < 4 else 6 * (d - 4)
        if sh:
            v(small(256), [nm], ["dgi%d" % d], ts(DI(d), src[:], sh, A_.arith_shift_right, 63, A_.bitwise_and))
        else:
            v(small(256), [nm], ["dgi%d" % d], ts(DI(d), src[:], 63, A_.bitwise_and))
        v(small(256), ["dgi%d" % d], ["dg%d" % d], ts(DG(d), DI(d), 0.5 if d % 2 == 0 else 32.0, A_.mult))
        dma("y", ["dg%d" % d], ["ptab%d" % d], T.ptab[d::16, :], DG(d), 2.5)
    PT = ["ptab%d" % d for d in range(6)]
    EV = ["tev0", "tev1"]

    v(small(512), ["sgi"], ["sgb"], cp(T.sgb[0:8, :], T.sgi[0:8, :]))
    op("p", 0.3, ["r8", "sgb"], ["vsl"], lambda q: q.matmul(T.vsl[:], T.r8[0:8, :], T.sgb[0:8, :], True, True), "vsl")
    v(small(512), ["vsl"], ["sgl"], cp(T.sgl[:], T.vsl[:]), "vsl")
    v(small(512), ["zi"], ["zf"], cp(T.zf[:], T.zi[:]))

    def slot(t, ci):
        return 192 * (2 * t + ci)

    for t in range(NV):
        cur[0] = "p"
        for ci, c in enumerate("AB"):
            B = lambda n, c=c: T[n + c]
            lanes = slice(L2 * ci, L2 * ci + L2)
            tl = slice(128 * t + L2 * ci, 128 * t + L2 * ci + L2)
            q0 = slot(t, ci)
            IS, IG, IR = T.inm[:, q0:q0 + 64], T.inm[:, q0 + 64:q0 + 128], T.inm[:, q0 + 128:q0 + 192]
            OX = T.oxm[:, 64 * (2 * t + ci):64 * (2 * t + ci) + 64]
            RX = T.rxm[:, 64 * (2 * t + ci):64 * (2 * t + ci) + 64]
            kS, kG, kR, kO = ["%s%d%s" % (n, t, c) for n in ("iS", "iG", "iR", "ox")]
            if t == 0:
                v(small(64), ["zi"], [kO], cp(OX, T.zi[:, tl]))
                v(small(64), ["si"], [kS], cp(IS, T.si[:, lanes]))
                v(small(64), ["gi"], [kG], cp(IG, T.gi[:, lanes]))
                v(small(64), ["sgl"], ["pos" + c], cp(B("pos")[:], T.sgl[:, tl]))
            else:
                kX = "rx%d%s" % (t, c)
                v(small(64), [kX], ["rxf" + c], cp(B("rxf")[:], RX))
                v(small(128), ["rxf" + c, "zf"], ["drz" + c], tt(B("drz")[:], B("rxf")[:], T.zf[:, tl], A_.subtract))
                v(small(64), [kR], ["om" + c], ts(B("om")[:], IR, -1.0, A_.mult, 1.0, A_.add))
                vx = T.vsl[:, 256 * ci + 128:256 * ci + 192]
                v(small(128), ["om" + c, "drz" + c], ["va" + c], tt(vx, B("om")[:], B("drz")[:], A_.mult), "vsl")
                v(small(64), ["va" + c, "rxf" + c], ["xf" + c], tt(B("xf")[:], B("rxf")[:], vx, A_.subtract), "vsl")
                v(small(64), ["xf" + c], [kO], cp(OX, B("xf")[:]))
                v(small(128), ["om" + c, "sgl"], ["pos" + c], tt(B("pos")[:], B("om")[:], T.sgl[:, tl], A_.mult))
            if t < NV - 1:
                op("net", 1.2, [kO], ["rx%d%s" % (t + 1, c)], ("x", t + 1, ci, OX), None, 6.0)
            op("s", gath(512), EV + [kO], ["exs" + c], act(B("ex")[:, 512:1024], T.tev[:].indirect(OX[:, 32:64]), F_.Copy))
            if ci in XV:
                v(gath(512), EV + [kO], ["exv" + c], cp(B("ex")[:, 0:512], T.tev[:].indirect(OX[:, 0:32])))
            else:
                op("s", gath(512), EV + [kO], ["exv" + c], act(B("ex")[:, 0:512], T.tev[:].indirect(OX[:, 0:32]), F_.Copy))
            v(small(64), [kS], ["Sf" + c], cp(B("sgf")[:, 0:64], IS))
            v(small(64), [kG], ["Gf" + c], cp(B("sgf")[:, 64:128], IG))
            for h in range(2):
                op("s", 0.07, ["pos" + c], ["nq" + c], act(B("nq")[:, :, h], B("pos")[:], F_.Copy, 2.0, -1.0))
                v(small(64), [kG, "fc13"], ["pg" + c], ts(B("pg")[:, :, h], IG, FC(13) if h == 0 else FC(3), A_.mult))
            op("s", 0.07, ["pos" + c], ["p2" + c], act(B("p2")[:], B("pos")[:], F_.Copy, 0.0, 2.0))
            op("p", 384 * PEC, ["pg" + c, "cg", "nq" + c, "cnb", "one", "c128"], ["gE" + c],
               mms([(B("pa")[:, 3], B("pg")[:], T.cg[:]), (B("pa")[:, 3], B("nq")[:], T.cnb[:]), (B("pa")[:, 3], T.one[:], T.c128[:])]), "pa" + c)
        if t > 0:
            op("p", 0.1, ["omA", "omB", "one"], ["par"],
               mms([(T.trA[:, 320:384], T.one[:], T.omA[:]), (T.trA[:, 320:384], T.one[:], T.omB[:])]), "trA")
            v(small(64), ["par"], ["cnt"], lambda q, t=t: q.tensor_reduce(T.cnt[:, t:t + 1], T.trA[:, 320:384], AxisListType.X, A_.add), "trA")
            v(small(1), ["cnt"], ["cni"], cp(T.cni[:, t:t + 1], T.cnt[:, t:t + 1]))
            v(small(1), ["cni"], ["cnj"], ts(T.cni[:, 8 + t:9 + t], T.cni[:, t:t + 1], 16, A_.bitwise_and))
            TB = lambda j, t=t: T.thb[:, 4 * t + j:4 * t + j + 1]
            for j, (m, b) in ((1, (-0.0625, 21.5)), (0, (0.0625, 11.0))):
                v(small(1), ["cnj"], ["th%d%d" % (t, j)], ts(TB(j), T.cni[:, 8 + t:9 + t], m, A_.mult, b, A_.add))
            for j, m in ((2, 1.5), (3, 2.0)):
                k = "th%d%d" % (t, j)
                v(small(1), ["cnj"], [k], ts(TB(j), T.cni[:, 8 + t:9 + t], -m * E11 / 16, A_.mult, m * E11, A_.add))
                v(small(1), [k], [k], ts(TB(j), TB(j), m * E12, A_.max))
        TH = lambda j, t=t: T.thb[:, 4 * t + j:4 * t + j + 1]
        for i in range(STEPS):
            cur[0] = str(i)
            for ci, c in enumerate("AB"):
                B = lambda n, c=c: T[n + c]
                q0 = slot(t, ci)
                off, kF = (T.inm[:, q0:q0 + 64], "iS%d%s" % (t, c)) if i == 0 else (B("off"), "off" + c)
                for a, b in cuts(CUT_P0 if i == 0 else CUT_P):
                    op("s", gath(16 * (b - a)), PT + [kF], ["gp" + c],
                       act(B("gp")[:, 16 * a:16 * b], T.ptab[:].indirect(off[:, a:b]), F_.Copy))
                for a, b in cuts((CUT_A, CUT_B)[ci]):
                    v(gath(16 * (b - a)), EV + [kF, "exs" + c, "exv" + c], ["ge" + c],
                      tt(B("ge")[:, 16 * a:16 * b], T.tev[:].indirect(off[:, a:b]), B("ex")[:, 16 * a:16 * b], A_.is_ge))
                op("p", 512 * PEC, ["gp" + c, "wp"], ["pa" + c],
                   mmk([(B("pa")[:, 0:3, :, k], B("gp")[:, k::8], T.wp[:]) for k in range(8)]), "pa" + c)
                op("p", 128 * PEC, ["nq" + c, "cna"], ["cw" + c], mms([(B("cv")[:, 0:2], B("nq")[:], T.cna[:])], True, False), "cv" + c)
                op("p", 512 * PEC, ["cw" + c, "ge" + c, "bo"], ["cv" + c],
                   mms([(B("cv")[:, 0:2, :, k], B("ge")[:, k::8], T.bo[:]) for k in range(8)], False, True), "cv" + c)
                op("s", 0.08, ["cv" + c], ["cz0" + c], act(B("cz")[:, 0], B("cv")[:, 0], F_.Sign, -7.5), "cv" + c)
                op("s", 0.08, ["cv" + c, "th%d1" % t], ["cz1" + c], act(B("cz")[:, 1], B("cv")[:, 1], F_.Sign, TH(1), -1.0), "cv" + c)
                VE, VD = T.vsl[:, 256 * ci:256 * ci + 64], T.vsl[:, 256 * ci + 64:256 * ci + 128]
                v(small(64), ["cz0" + c, "pa" + c], ["tu" + c], tt(B("tu")[:], B("cz")[:, 0], B("pa")[:, 0], A_.mult), "pa" + c)
                NX, MV = B("zz")[:, 1::2, :], B("zm")[:, 1::2, :]
                v(small(64), ["tu" + c, "pa" + c], ["zz" + c], tt(NX, B("tu")[:], B("pa")[:, 1], A_.add), "pa" + c)
                op("p", 512 * PEC, ["zz" + c, "ch0", "ch1"], ["aN" + c],
                   mms([(B("tr")[:, 0:64], B("zz")[:, 1:17, :], T.ch0[:]), (B("tr")[:, 0:64], B("zz")[:, 0:16, :], T.ch1[:])], True, False), "tr" + c)
                v(small(64), ["zz" + c, "gE" + c], ["ve" + c], tt(VE, NX, B("pa")[:, 3], A_.is_equal), "pa" + c)
                v(small(64), ["zz" + c, "pa" + c], ["vd" + c], tt(VD, B("pa")[:, 2], NX, A_.subtract), "pa" + c)
                v(small(64), ["ve" + c, "cz1" + c], ["mx" + c], tt(B("mx")[:], B("cz")[:, 1], VE, A_.max))
                v(small(64), ["mx" + c, "vd" + c], ["zm" + c], tt(MV, B("mx")[:], VD, A_.mult))
                if i == STEPS - 1:
                    v(small(64), ["mx" + c, "cv" + c], ["zk" + c], tt(B("zk")[:, 1::2, :], B("mx")[:], B("cv")[:, 1], A_.mult), "cv" + c)
                op("p", 512 * PEC, ["zm" + c, "aN" + c, "ch0", "ch1"], ["aL" + c],
                   mms([(B("tr")[:, 0:64], B("zm")[:, 1:17, :], T.ch0[:]), (B("tr")[:, 0:64], B("zm")[:, 0:16, :], T.ch1[:])], False, True), "tr" + c)
                if i < STEPS - 1:
                    v(small(64), ["aL" + c], ["off" + c], cp(B("off")[:], B("tr")[:, 0:64]), "tr" + c)
            if i == 0:
                cur[0] = "g"
                for ci, c in enumerate("AB"):
                    B = lambda n, c=c: T[n + c]
                    q0 = slot(t, ci) + 64
                    for a, b in cuts(CUT_G):
                        v(gath(16 * (b - a)), EV + ["iG%d%s" % (t, c), "exs" + c, "exv" + c], ["gg" + c],
                          tt(B("gg")[:, 16 * a:16 * b], T.tev[:].indirect(T.inm[:, q0 + a:q0 + b]), B("ex")[:, 16 * a:16 * b], A_.is_ge))
                    CG, FM = T.gl[:, 128 * ci:128 * ci + 64], T.gl[:, 128 * ci + 64:128 * ci + 128]
                    op("p", 1024 * PEC, ["gg" + c, "w0"], ["cG" + c],
                       mms([(CG, T.w0[:, 16 - k:144 - k], B("gg")[:, k::16]) for k in range(16)]), "gl")
                    v(small(64), ["cG" + c, "th%d0" % t], ["mi" + c], ts(B("mi")[:], CG, TH(0), A_.is_lt), "gl")
                    op("p", 0.1, ["mi" + c, "p2" + c, "blk"], ["fm" + c],
                       mms([(FM, T.blk[:], B("mi")[:]), (FM, T.blk[:], B("p2")[:])]), "gl")
                    v(small(64), ["fm" + c], ["fu" + c], ts(B("fu")[:], FM, 0.0, A_.is_equal), "gl")
                    v(small(64), ["fm" + c], ["pu" + c], ts(B("pu")[:], FM, 36.0, A_.is_gt), "gl")
                    v(small(64), ["fm" + c], ["nf" + c], ts(B("nf")[:], FM, 0.0, A_.is_gt, -64.0, A_.mult), "gl")
        cur[0] = "f"
        for ci, c in enumerate("AB"):
            B = lambda n, c=c: T[n + c]
            bk, bg = "tr" + c, "gl"
            KL, MM, AL = T.gl[:, 256 + 128 * ci:320 + 128 * ci], T.gl[:, 320 + 128 * ci:384 + 128 * ci], B("tr")[:, 0:64]
            va, vb, vm = [T.vsl[:, 256 * ci + 64 * j:256 * ci + 64 * j + 64] for j in (2, 3, 0)]
            Sf, Gf = B("sgf")[:, 0:64], B("sgf")[:, 64:128]
            so = T.som[:, slot(t, ci):slot(t, ci) + 192]
            kM = "so%d%s" % (t, c)
            op("p", 0.15, ["zk" + c, "nf" + c, "cb0", "cb1", "idb"], ["kL" + c],
               mms([(KL, B("zk")[:, 1:17, :], T.cb0[:]), (KL, B("zk")[:, 0:16, :], T.cb1[:]), (KL, T.idb[:], B("nf")[:])]), bg)
            op("s", 0.08, ["kL" + c, "fc14"], ["ww" + c], act(B("ww")[:], KL, F_.Exp, FC(14), 16 * ALPHA), bg)
            op("p", 0.1, ["ww" + c, "blk"], ["MM" + c], mms([(MM, T.blk[:], B("ww")[:])]), bg)
            v(small(64), ["MM" + c, "th%d2" % t], ["ve" + c], ts(vm, MM, 0.5, A_.mult, TH(2), A_.max), bg)
            if t < NV - 1:
                v(small(64), ["MM" + c, "th%d3" % t], ["nc" + c], ts(B("nc")[:], MM, TH(3), A_.is_lt), bg)
            v(small(64), ["aL" + c, "Sf" + c], ["va" + c], tt(va, AL, Sf, A_.subtract), bk)
            v(small(64), ["va" + c, "pos" + c], ["va" + c], tt(va, B("pos")[:], va, A_.mult))
            v(small(64), ["va" + c, "Sf" + c], ["stS" + c], tt(B("st")[:, 0:64], Sf, va, A_.add))
            v(small(64), ["stS" + c], [kM + "S"], cp(so[:, 0:64], B("st")[:, 0:64]))
            v(small(64), ["aL" + c, "Gf" + c], ["vb" + c], tt(vb, AL, Gf, A_.subtract), bk)
            vp = T.vsl[:, 256 * ci + 64:256 * ci + 128]
            v(small(64), ["vb" + c, "pu" + c], ["vd" + c], tt(vp, B("pu")[:], vb, A_.mult))
            v(small(64), ["vd" + c, "Gf" + c], ["upd" + c], tt(B("upd")[:], Gf, vp, A_.add))
            v(small(64), ["ve" + c, "ww" + c], ["hit" + c], tt(B("hit")[:], B("ww")[:], vm, A_.is_gt))
            if t < NV - 1:
                v(small(128), ["nc" + c, "fu" + c], ["stR" + c], tt(B("st")[:, 128:192], B("nc")[:], B("fu")[:], A_.mult))
            v(small(64), ["hit" + c, "vb" + c], ["vb" + c], tt(vb, B("hit")[:], vb, A_.mult))
            v(small(64), ["vb" + c, "upd" + c], ["stG" + c], tt(B("st")[:, 64:128], B("upd")[:], vb, A_.add))
            nw = 192 if t < NV - 1 else 128
            v(small(nw - 64), ["stG" + c] + (["stR" + c] if t < NV - 1 else []), [kM], cp(so[:, 64:nw], B("st")[:, 64:nw]))
            op("net", 1.2, [kM, kM + "S"], ["%s%d%s" % (n, t + 1, c) for n in ("iS", "iG", "iR")],
               ("m", t + 1, ci, so[:, 0:nw]), None, 6.0)
    for ci, c in enumerate("AB"):
        q0 = slot(NV, ci)
        for j in range(2):
            v(small(64), ["iS4" + c], ["yo%d%s" % (j, c)], cp(T.yo[:, 128 * j + 64 * ci:128 * j + 64 * ci + 64], T.inm[:, q0 + 64 * j:q0 + 64 * j + 64]))
            dma("ys"[j], ["yo%d%s" % (j, c)], [], (T.ys, T.yg)[j][:, 64 * ci:64 * ci + 64], T.yo[:, 128 * j + 64 * ci:128 * j + 64 * ci + 64], 2.0)
    return ops


def link(ops):
    wr, rd, base, bank = {}, {}, {}, {}
    for n, o in enumerate(ops):
        d = set()
        for k in o["R"]:
            d.update(wr.get(k, ()))
        for k in o["W"]:
            old = wr.get(k, [])
            piece = old and k not in o["R"] and not rd.get(k) and all(ops[m]["e"] == o["e"] and ops[m]["W"] == o["W"] for m in old)
            if piece:
                wr[k] = old + [n]
            else:
                base[k] = set(old) | set(rd.get(k, ()))
                wr[k] = [n]
                rd[k] = []
            d.update(base[k])
        if o["b"]:
            sg = bank.get(o["b"])
            if not sg or sg["e"] != o["e"]:
                sg = bank[o["b"]] = {"e": o["e"], "n": [], "pre": set(sg["n"]) if sg else set()}
            d.update(sg["pre"])
            sg["n"].append(n)
        d.discard(n)
        o["D"] = sorted(d)
        for k in o["R"]:
            if k not in o["W"]:
                rd.setdefault(k, []).append(n)
    return ops


def order(ops):
    n = len(ops)
    suc = [[] for _ in ops]
    pri = [0.0] * n
    need = [len(o["D"]) for o in ops]
    for i, o in enumerate(ops):
        for d in o["D"]:
            suc[d].append(i)
    for i in range(n - 1, -1, -1):
        o = ops[i]
        pri[i] = o["c"] + o["lat"] + LAT + max([pri[j] for j in suc[i]] or [0.0])
    for i in range(n):
        pri[i] += SHIFT.get(ops[i]["key"], 0.0)
    free, ready, est, done, seq = {}, [], [0.0] * n, [0.0] * n, []
    ready = [i for i in range(n) if not need[i]]
    q = lambda e: "g" if e == "net" else e
    while ready:
        tm = min(max(est[i], free.get(q(ops[i]["e"]), 0.0)) for i in ready)
        first = min((max(est[i], free.get(q(ops[i]["e"]), 0.0)), -pri[i], i) for i in ready)
        eng = q(ops[first[2]]["e"])
        cand = [i for i in ready if q(ops[i]["e"]) == eng and max(est[i], free.get(eng, 0.0)) <= tm + 0.02]
        b = max(cand, key=lambda i: (pri[i], -i))
        s = max(est[b], free.get(eng, 0.0))
        free[eng] = s + ops[b]["c"]
        done[b] = s + ops[b]["c"] + ops[b]["lat"]
        ready.remove(b)
        seq.append(b)
        for j in suc[b]:
            need[j] -= 1
            est[j] = max(est[j], done[b] + LAT)
            if not need[j]:
                ready.append(j)
    return seq


def emit(g, core, T, topo, ops, seq, nxt, home):
    qs = {"v": g.vector, "s": g.scalar, "p": g.tensor, "g": g, "net": g, "y": g.sync}
    cs = {"v": "v", "s": "s", "p": "p", "g": "q"}
    known = {e: {} for e in "vspgy"}
    count = {}
    loc = 0
    for n in seq:
        o = ops[n]
        e = "g" if o["e"] == "net" else o["e"]
        q, kn = qs[e], known[e]
        for d in o["D"]:
            for sem, val, clk in ops[d]["sig"]:
                if kn.get(sem, 0) < val:
                    q.wait_ge(T.sem[sem], val)
                    kn[sem] = val
                    for k2, v2 in clk.items():
                        if kn.get(k2, 0) < v2:
                            kn[k2] = v2
        if o["e"] == "net":
            kind, t, ci, src = o["f"]
            dst = home if t == NV else nxt
            via = routes(core, dst, topo)[ci]
            to = dst if via == core else via
            sem = ("arr%d%s" if kind == "m" else "xar%d%s") % (t, "AB"[ci])
            wide = 192 if kind == "m" else 64
            w = 128 if kind == "m" and t == NV else wide
            at = wide * (2 * t + ci)
            land = (T.inm if kind == "m" else T.rxm)[:, at:at + w]
            rid, pid = topo.addr(to, core)
            g.remote_dma(land, src, T.sem[sem], T.sem.loc, pid, rid, topo.mask(core, to))
            loc += len(topo.engines(core, to))
            o["sig"] = [(sem, last_hop(T, core, t, kind, ci, topo), {})]
        elif "dsem" in o:
            o["f"](q).then_inc(T.sem[o["dsem"]], 16)
            o["sig"] = [(o["dsem"], 16, dict(kn))]
        else:
            sem = cs[e]
            count[sem] = count.get(sem, 0) + 1
            o["f"](q).then_inc(T.sem[sem], 1)
            clk = dict(kn)
            clk[sem] = count[sem]
            o["sig"] = [(sem, count[sem], clk)]
    for o in ops:
        if "dsem" in o:
            g.wait_ge(T.sem[o["dsem"]], 16)
    for sem, val in count.items():
        g.wait_ge(T.sem[sem], val)
    g.wait_ge(T.sem.loc, loc)


def ends(rank, T, kind, t):
    n = len(T.cores)
    return (rank - (NV - 1)) % n if t == NV else (rank + 1) % n


def last_hop(T, core, t, kind, ci, topo):
    rank, n = T.rank_of(core), len(T.cores)
    src = T.cores[(rank + (NV - 1)) % n] if t == NV else T.cores[(rank - 1) % n]
    via = routes(src, core, topo)[ci]
    return len(topo.engines(via, core))


def relay(g, core, T, topo):
    jobs = []
    for rank, src in enumerate(T.cores):
        if core not in topo.cores_of(src):
            continue
        for t in range(1, NV + 1):
            dst = T.cores[ends(rank, T, "m", t)]
            for ci in range(NC):
                if routes(src, dst, topo)[ci] == core:
                    if t < NV:
                        jobs.append((src, dst, t, 0, ci))
                    jobs.append((src, dst, t, 1, ci))
    jobs.sort(key=lambda j: (j[2], j[3], j[4]))
    loc = 0
    for src, dst, t, m, ci in jobs:
        wide = 192 if m else 64
        w = 128 if m and t == NV else wide
        at = wide * (2 * t + ci)
        sem = T.sem[("arr%d%s" if m else "xar%d%s") % (t, "AB"[ci])]
        buf = (T.inm if m else T.rxm)[:, at:at + w]
        g.wait_ge(sem, len(topo.engines(src, core)))
        rid, pid = topo.addr(dst, core)
        g.remote_dma(buf, buf, sem, T.sem.loc, pid, rid, topo.mask(core, dst))
        loc += len(topo.engines(core, dst))
    if loc:
        g.wait_ge(T.sem.loc, loc)


def rank_program(g, core, T, topo):
    rank = T.rank_of(core)
    if rank is None:
        relay(g, core, T, topo)
        return
    ops = link(build(T))
    seq = order(ops)
    emit(g, core, T, topo, ops, seq, T.cores[ends(rank, T, "m", 1)], T.cores[ends(rank, T, "m", NV)])
